import numpy as np
import ml_dtypes


def mxq(x, axis, fmt="e4m3"):
    dtype, down = {"e4m3": (ml_dtypes.float8_e4m3fn, 7), "e5m2": (ml_dtypes.float8_e5m2, 14)}[fmt]
    v = np.moveaxis(np.asarray(x, np.float32).astype(ml_dtypes.bfloat16).astype(np.float64), axis, -1)
    blocks = v.reshape(v.shape[:-1] + (-1, 32))
    amax = np.abs(blocks).max(-1, keepdims=True)
    byte = np.maximum(np.where(amax > 0, np.frexp(amax)[1] - 1 + 127, 0) - down, 1)
    scale = np.exp2(byte - 127.0)
    codes = (blocks / scale).astype(np.float32).astype(dtype).astype(np.float64)
    return np.moveaxis((codes * scale).reshape(v.shape), -1, axis)


WIDE = False


def mx_kscale(k):
    if not WIDE:
        return np.ones(k)
    levels = np.array([10, -10, 5, -5, 0])
    if k % 512:
        return np.exp2(np.random.permutation(np.resize(levels, k // 32))).repeat(32)
    a = np.empty((k // 512, 16))
    for p in range(k // 512):
        a[p, :8] = np.random.permutation(np.resize(levels, 8))
        for g in range(8):
            far = levels[np.abs(levels - a[p, g]) >= 10]
            a[p, g + 8] = far[np.random.randint(len(far))]
    return np.exp2(a.ravel()).repeat(32)


def f64(x):
    return np.asarray(x).astype(np.float64)


def striped(idx):
    return np.tile(idx.reshape(-1, 16).T, (8, 1)).astype(np.uint16)


def unstriped(offs):
    return offs[:16].T.reshape(-1).astype(np.int64)


def pack_weight(w):
    k, n = w.shape
    w = f64(np.asarray(w, np.float32).astype(ml_dtypes.bfloat16)).reshape(k // 32, 32, n)
    amax = np.abs(w).max(1)
    byte = np.clip(np.where(amax > 0, np.frexp(amax)[1] - 1 + 127 - 7, 1), 1, 254)
    scaled = (w * np.exp2(127.0 - byte)[:, None, :]).reshape(k, n).astype(np.float32)
    words = np.ascontiguousarray(scaled.reshape(k // 512, 128, 4, n).transpose(0, 1, 3, 2)).astype(ml_dtypes.float8_e4m3fn).view(np.uint8)
    return words, np.ascontiguousarray(byte.astype(np.uint8).reshape(k // 512, 16, n))


def unpack_weight(words, scales):
    g, p, n, _ = words.shape
    vals = np.ascontiguousarray(words).view(ml_dtypes.float8_e4m3fn).astype(np.float64) * np.repeat(np.exp2(scales.astype(np.float64) - 127.0), 8, axis=1)[..., None]
    return vals.transpose(0, 1, 3, 2).reshape(g * 512, n)


K, T, S, N, U = 512, 1024, 512, 256, 1024


def setup_inputs():
    n = np.random.standard_normal
    s = mx_kscale(K)[:, None]
    packed_w1 = pack_weight(n((K, N)) / np.sqrt(K) / s)
    return {
        "xT": (n((K, T)) * s).astype(np.float32),
        "mem": n((N, U)).astype(np.float32),
        "w1_words": packed_w1[0],
        "w1_scales": packed_w1[1],
        "offs": striped(np.random.permutation(T)[:S]),
        "slot": striped(np.random.permutation(U)[:S]),
    }


def reference(xT, mem, w1_words, w1_scales, offs, slot):
    xq = mxq(f64(xT)[:, unstriped(offs)], 0, "e4m3")
    y = unpack_weight(w1_words, w1_scales).T @ xq
    out = f64(mem).copy()
    out[:, unstriped(slot)] = np.maximum(f64(mem)[:, unstriped(slot)], y)
    return out

@@ -1,0 +1,81 @@
+from contextlib import ExitStack
+
+import concourse.mybir as mybir
+
+K, T, S, N, U = 512, 1024, 512, 256, 1024
+P = 128
+FLOPS = 2 * K * S * N
+
+F32 = mybir.dt.float32
+BF16 = mybir.dt.bfloat16
+I32 = mybir.dt.int32
+U32 = mybir.dt.uint32
+U16 = mybir.dt.uint16
+U8 = mybir.dt.uint8
+FP8X4 = mybir.dt.float8_e4m3fn_x4
+COPY = mybir.ActivationFunctionType.Copy
+MAX = mybir.AluOpType.max
+
+
+def tile_picked_idxput_max_e_kernel(tc, xT, mem, w1_words, w1_scales, offs, slot, out):
+    nc = tc.nc
+    H = T // 2
+    with ExitStack() as ctx:
+        keep = ctx.enter_context(tc.tile_pool(name="keep", bufs=1))
+        psum = ctx.enter_context(tc.psum_pool(name="psum", bufs=1))
+
+        offs_sb = keep.tile([P, S // 16], U16, name="offs_sb")
+        slot_sb = keep.tile([P, S // 16], U16, name="slot_sb")
+        w_codes = keep.tile([P, N], U32, name="w_codes", align_bytes=64)
+        w_scale = keep.tile([P, N], U8, name="w_scale", align_bytes=64)
+        row2 = keep.tile([P, T], F32, name="row2")
+        row3 = [keep.tile([P, H], F32, name=f"row3_{h}") for h in range(2)]
+        rows01 = [keep.tile([P, 2, H], F32, name=f"rows01_{h}") for h in range(2)]
+        store = [keep.tile([P, U], F32, name=f"store{b}") for b in range(2)]
+        pair = keep.tile([P, T, 2], BF16, name="pair")
+        row2_bf = keep.tile([P, T], BF16, name="row2_bf")
+        row3_bf = keep.tile([P, T], BF16, name="row3_bf")
+        picked = keep.tile([P, S, 4], BF16, name="picked", align_bytes=64)
+        x_codes = keep.tile([P, S], U32, name="x_codes", align_bytes=64)
+        x_scale = keep.tile([P, S], U8, name="x_scale", align_bytes=64)
+        old = [keep.tile([P, S], F32, name=f"old{b}") for b in range(2)]
+        new = [keep.tile([P, S], F32, name=f"new{b}") for b in range(2)]
+
+        nc.vector.memset(w_scale[:].bitcast(I32), 0)
+
+        xv = xT.rearrange("(p j) t -> p j t", j=4)
+        nc.sync.dma_start(row2[:], xv[:, 2, :])
+        nc.sync.dma_start(offs_sb[:], offs)
+        for h in range(2):
+            nc.sync.dma_start(rows01[h][:], xv[:, 0:2, h * H:(h + 1) * H])
+        for h in range(2):
+            nc.sync.dma_start(row3[h][:], xv[:, 3, h * H:(h + 1) * H])
+        nc.sync.dma_start(slot_sb[:], slot)
+        nc.sync.dma_start(store[0][:], mem[0:P, :])
+        nc.sync.dma_start(w_codes[:].bitcast(I32), w1_words[0].rearrange("p n t -> p (n t)").bitcast(I32))
+        for q in range(4):
+            nc.sync.dma_start(w_scale[32 * q:32 * q + 4, :].bitcast(I32), w1_scales[0, 4 * q:4 * q + 4, :].bitcast(I32))
+        nc.sync.dma_start(store[1][:], mem[P:2 * P, :])
+
+        nc.scalar.copy(row2_bf[:], row2[:])
+        nc.scalar.activation(picked[:, :, 2], row2_bf[:].indirect(offs_sb[:]), COPY)
+        for h in range(2):
+            nc.vector.tensor_copy(pair[:, h * H:(h + 1) * H, :], rows01[h][:].rearrange("p j t -> p t j"))
+        pair_words = pair[:].rearrange("p t j -> p (t j)").bitcast(U32)
+        picked_words = picked[:].rearrange("p s j -> p (s j)").bitcast(U32).rearrange("p (s u) -> p s u", u=2)
+        nc.vector.tensor_copy(picked_words[:, :, 0], pair_words.indirect(offs_sb[:]))
+        for h in range(2):
+            nc.scalar.copy(row3_bf[:, h * H:(h + 1) * H], row3[h][:])
+        nc.scalar.activation(picked[:, :, 3], row3_bf[:].indirect(offs_sb[:]), COPY)
+
+        nc.vector.tensor_copy(old[0][:], store[0][:].indirect(slot_sb[:]))
+        nc.vector.quantize_mx(out=x_codes[:].bitcast(FP8X4), scales=x_scale[:], in_=picked[:].rearrange("p s j -> p (s j)"))
+        nc.vector.tensor_copy(old[1][:], store[1][:].indirect(slot_sb[:]))
+        for b in range(2):
+            acc = psum.tile([P, S], F32, name=f"acc{b}")
+            nc.tensor.matmul_mx(out=acc[:], lhsT=w_codes[:, b * P:(b + 1) * P].bitcast(FP8X4), lhsT_scale=w_scale[:, b * P:(b + 1) * P],
+                                rhs=x_codes[:].bitcast(FP8X4), rhs_scale=x_scale[:], start=True, stop=True)
+            nc.vector.tensor_tensor(new[b][:], acc[:], old[b][:], MAX)
+        for b in range(2):
+            nc.vector.tensor_copy(store[b][:].indirect(slot_sb[:]), new[b][:])
+            nc.sync.dma_start(out[b * P:(b + 1) * P, :], store[b][:])

@@ -35,9 +35,10 @@ def tile_picked_idxput_max_e_kernel(tc, xT, mem, w1_words, w1_scales, offs, slot
         pair = keep.tile([P, T, 2], BF16, name="pair")
         row2_bf = keep.tile([P, T], BF16, name="row2_bf")
         row3_bf = keep.tile([P, T], BF16, name="row3_bf")
-        picked = keep.tile([P, S, 4], BF16, name="picked", align_bytes=64)
-        x_codes = keep.tile([P, S], U32, name="x_codes", align_bytes=64)
-        x_scale = keep.tile([P, S], U8, name="x_scale", align_bytes=64)
+        SH = S // 2
+        picked = [keep.tile([P, SH, 4], BF16, name=f"picked{h}", align_bytes=64) for h in range(2)]
+        x_codes = [keep.tile([P, SH], U32, name=f"x_codes{h}", align_bytes=64) for h in range(2)]
+        x_scale = [keep.tile([P, SH], U8, name=f"x_scale{h}", align_bytes=64) for h in range(2)]
         old = [keep.tile([P, S], F32, name=f"old{b}") for b in range(2)]
         new = [keep.tile([P, S], F32, name=f"new{b}") for b in range(2)]
 
@@ -48,34 +49,45 @@ def tile_picked_idxput_max_e_kernel(tc, xT, mem, w1_words, w1_scales, offs, slot
         nc.sync.dma_start(offs_sb[:], offs)
         for h in range(2):
             nc.sync.dma_start(rows01[h][:], xv[:, 0:2, h * H:(h + 1) * H])
-        for h in range(2):
-            nc.sync.dma_start(row3[h][:], xv[:, 3, h * H:(h + 1) * H])
         nc.sync.dma_start(slot_sb[:], slot)
         nc.sync.dma_start(store[0][:], mem[0:P, :])
+        for h in range(2):
+            nc.sync.dma_start(row3[h][:], xv[:, 3, h * H:(h + 1) * H])
+        nc.sync.dma_start(store[1][:], mem[P:2 * P, :])
         nc.sync.dma_start(w_codes[:].bitcast(I32), w1_words[0].rearrange("p n t -> p (n t)").bitcast(I32))
         for q in range(4):
             nc.sync.dma_start(w_scale[32 * q:32 * q + 4, :].bitcast(I32), w1_scales[0, 4 * q:4 * q + 4, :].bitcast(I32))
-        nc.sync.dma_start(store[1][:], mem[P:2 * P, :])
 
-        nc.scalar.copy(row2_bf[:], row2[:])
-        nc.scalar.activation(picked[:, :, 2], row2_bf[:].indirect(offs_sb[:]), COPY)
+        half = [offs_sb[:, h * (SH // 16):(h + 1) * (SH // 16)] for h in range(2)]
+        nc.scalar.copy(row2_bf[:, 0:320], row2[:, 0:320])
+        nc.vector.tensor_copy(row2_bf[:, 320:T], row2[:, 320:T])
+        for h in range(2):
+            nc.scalar.activation(picked[h][:, :, 2], row2_bf[:].indirect(half[h]), COPY)
         for h in range(2):
             nc.vector.tensor_copy(pair[:, h * H:(h + 1) * H, :], rows01[h][:].rearrange("p j t -> p t j"))
         pair_words = pair[:].rearrange("p t j -> p (t j)").bitcast(U32)
-        picked_words = picked[:].rearrange("p s j -> p (s j)").bitcast(U32).rearrange("p (s u) -> p s u", u=2)
-        nc.vector.tensor_copy(picked_words[:, :, 0], pair_words.indirect(offs_sb[:]))
+        for h in range(2):
+            picked_words = picked[h][:].rearrange("p s j -> p (s j)").bitcast(U32).rearrange("p (s u) -> p s u", u=2)
+            nc.vector.tensor_copy(picked_words[:, :, 0], pair_words.indirect(half[h]))
+        nc.vector.tensor_copy(old[0][:], store[0][:].indirect(slot_sb[:]))
         for h in range(2):
             nc.scalar.copy(row3_bf[:, h * H:(h + 1) * H], row3[h][:])
-        nc.scalar.activation(picked[:, :, 3], row3_bf[:].indirect(offs_sb[:]), COPY)
-
-        nc.vector.tensor_copy(old[0][:], store[0][:].indirect(slot_sb[:]))
-        nc.vector.quantize_mx(out=x_codes[:].bitcast(FP8X4), scales=x_scale[:], in_=picked[:].rearrange("p s j -> p (s j)"))
+        for h in range(2):
+            nc.scalar.activation(picked[h][:, :, 3], row3_bf[:].indirect(half[h]), COPY)
         nc.vector.tensor_copy(old[1][:], store[1][:].indirect(slot_sb[:]))
-        for b in range(2):
-            acc = psum.tile([P, S], F32, name=f"acc{b}")
-            nc.tensor.matmul_mx(out=acc[:], lhsT=w_codes[:, b * P:(b + 1) * P].bitcast(FP8X4), lhsT_scale=w_scale[:, b * P:(b + 1) * P],
-                                rhs=x_codes[:].bitcast(FP8X4), rhs_scale=x_scale[:], start=True, stop=True)
-            nc.vector.tensor_tensor(new[b][:], acc[:], old[b][:], MAX)
+
+        for h in range(2):
+            nc.vector.quantize_mx(out=x_codes[h][:].bitcast(FP8X4), scales=x_scale[h][:], in_=picked[h][:].rearrange("p s j -> p (s j)"))
+        acc = {}
+        for h in range(2):
+            for b in range(2):
+                acc[b, h] = psum.tile([P, SH], F32, name=f"acc{b}{h}")
+                nc.tensor.matmul_mx(out=acc[b, h][:], lhsT=w_codes[:, b * P:(b + 1) * P].bitcast(FP8X4), lhsT_scale=w_scale[:, b * P:(b + 1) * P],
+                                    rhs=x_codes[h][:].bitcast(FP8X4), rhs_scale=x_scale[h][:], start=True, stop=True)
+        for h in range(2):
+            for b in range(2):
+                cols = slice(h * SH, (h + 1) * SH)
+                nc.vector.tensor_tensor(new[b][:, cols], acc[b, h][:], old[b][:, cols], MAX)
         for b in range(2):
             nc.vector.tensor_copy(store[b][:].indirect(slot_sb[:]), new[b][:])
             nc.sync.dma_start(out[b * P:(b + 1) * P, :], store[b][:])

@@ -19,7 +19,10 @@ MAX = mybir.AluOpType.max
 
 def tile_picked_idxput_max_e_kernel(tc, xT, mem, w1_words, w1_scales, offs, slot, out):
     nc = tc.nc
-    H = T // 2
+    PIECES = [512]
+    starts = [sum(PIECES[:i]) for i in range(len(PIECES) + 1)]
+    cut01 = [0,640,1024]
+    cut3 = [0,512,1024]
     with ExitStack() as ctx:
         keep = ctx.enter_context(tc.tile_pool(name="keep", bufs=1))
         psum = ctx.enter_context(tc.psum_pool(name="psum", bufs=1))
@@ -29,16 +32,15 @@ def tile_picked_idxput_max_e_kernel(tc, xT, mem, w1_words, w1_scales, offs, slot
         w_codes = keep.tile([P, N], U32, name="w_codes", align_bytes=64)
         w_scale = keep.tile([P, N], U8, name="w_scale", align_bytes=64)
         row2 = keep.tile([P, T], F32, name="row2")
-        row3 = [keep.tile([P, H], F32, name=f"row3_{h}") for h in range(2)]
-        rows01 = [keep.tile([P, 2, H], F32, name=f"rows01_{h}") for h in range(2)]
+        row3 = [keep.tile([P, cut3[i + 1] - cut3[i]], F32, name=f"row3_{i}") for i in range(len(cut3) - 1)]
+        rows01 = [keep.tile([P, 2, cut01[i + 1] - cut01[i]], F32, name=f"rows01_{i}") for i in range(len(cut01) - 1)]
         store = [keep.tile([P, U], F32, name=f"store{b}") for b in range(2)]
         pair = keep.tile([P, T, 2], BF16, name="pair")
         row2_bf = keep.tile([P, T], BF16, name="row2_bf")
         row3_bf = keep.tile([P, T], BF16, name="row3_bf")
-        SH = S // 2
-        picked = [keep.tile([P, SH, 4], BF16, name=f"picked{h}", align_bytes=64) for h in range(2)]
-        x_codes = [keep.tile([P, SH], U32, name=f"x_codes{h}", align_bytes=64) for h in range(2)]
-        x_scale = [keep.tile([P, SH], U8, name=f"x_scale{h}", align_bytes=64) for h in range(2)]
+        picked = [keep.tile([P, n, 4], BF16, name=f"picked{i}", align_bytes=64) for i, n in enumerate(PIECES)]
+        x_codes = [keep.tile([P, n], U32, name=f"x_codes{i}", align_bytes=64) for i, n in enumerate(PIECES)]
+        x_scale = [keep.tile([P, n], U8, name=f"x_scale{i}", align_bytes=64) for i, n in enumerate(PIECES)]
         old = [keep.tile([P, S], F32, name=f"old{b}") for b in range(2)]
         new = [keep.tile([P, S], F32, name=f"new{b}") for b in range(2)]
 
@@ -47,47 +49,52 @@ def tile_picked_idxput_max_e_kernel(tc, xT, mem, w1_words, w1_scales, offs, slot
         xv = xT.rearrange("(p j) t -> p j t", j=4)
         nc.sync.dma_start(row2[:], xv[:, 2, :])
         nc.sync.dma_start(offs_sb[:], offs)
-        for h in range(2):
-            nc.sync.dma_start(rows01[h][:], xv[:, 0:2, h * H:(h + 1) * H])
+        nc.sync.dma_start(rows01[0][:], xv[:, 0:2, cut01[0]:cut01[1]])
+        nc.sync.dma_start(rows01[1][:], xv[:, 0:2, cut01[1]:cut01[2]])
         nc.sync.dma_start(slot_sb[:], slot)
-        nc.sync.dma_start(store[0][:], mem[0:P, :])
-        for h in range(2):
-            nc.sync.dma_start(row3[h][:], xv[:, 3, h * H:(h + 1) * H])
-        nc.sync.dma_start(store[1][:], mem[P:2 * P, :])
+        nc.sync.dma_start(row3[0][:], xv[:, 3, cut3[0]:cut3[1]])
+        nc.sync.dma_start(row3[1][:], xv[:, 3, cut3[1]:cut3[2]])
+        nc.sync.dma_start(store[0][:], mem[0 * P:1 * P, :])
+        nc.sync.dma_start(store[1][:], mem[1 * P:2 * P, :])
         nc.sync.dma_start(w_codes[:].bitcast(I32), w1_words[0].rearrange("p n t -> p (n t)").bitcast(I32))
         for q in range(4):
             nc.sync.dma_start(w_scale[32 * q:32 * q + 4, :].bitcast(I32), w1_scales[0, 4 * q:4 * q + 4, :].bitcast(I32))
 
-        half = [offs_sb[:, h * (SH // 16):(h + 1) * (SH // 16)] for h in range(2)]
+        part = [offs_sb[:, starts[i] // 16:starts[i + 1] // 16] for i in range(len(PIECES))]
         nc.scalar.copy(row2_bf[:, 0:320], row2[:, 0:320])
         nc.vector.tensor_copy(row2_bf[:, 320:T], row2[:, 320:T])
-        for h in range(2):
-            nc.scalar.activation(picked[h][:, :, 2], row2_bf[:].indirect(half[h]), COPY)
-        for h in range(2):
-            nc.vector.tensor_copy(pair[:, h * H:(h + 1) * H, :], rows01[h][:].rearrange("p j t -> p t j"))
+        for i in range(len(PIECES)):
+            nc.scalar.activation(picked[i][:, :, 2], row2_bf[:].indirect(part[i]), COPY)
+        nc.vector.tensor_copy(pair[:, 0:cut01[1], :], rows01[0][:].rearrange("p j t -> p t j"))
+        tail = rows01[1][:].rearrange("p j t -> p t j")
+        nc.vector.tensor_copy(pair[:, cut01[1]:T - 128, :], tail[:, 0:T - 128 - cut01[1], :])
+        nc.scalar.copy(pair[:, T - 128:T, :], tail[:, T - 128 - cut01[1]:T - cut01[1], :])
         pair_words = pair[:].rearrange("p t j -> p (t j)").bitcast(U32)
-        for h in range(2):
-            picked_words = picked[h][:].rearrange("p s j -> p (s j)").bitcast(U32).rearrange("p (s u) -> p s u", u=2)
-            nc.vector.tensor_copy(picked_words[:, :, 0], pair_words.indirect(half[h]))
+        for i in range(len(PIECES)):
+            picked_words = picked[i][:].rearrange("p s j -> p (s j)").bitcast(U32).rearrange("p (s u) -> p s u", u=2)
+            nc.vector.tensor_copy(picked_words[:, :, 0], pair_words.indirect(part[i]))
         nc.vector.tensor_copy(old[0][:], store[0][:].indirect(slot_sb[:]))
-        for h in range(2):
-            nc.scalar.copy(row3_bf[:, h * H:(h + 1) * H], row3[h][:])
-        for h in range(2):
-            nc.scalar.activation(picked[h][:, :, 3], row3_bf[:].indirect(half[h]), COPY)
-        nc.vector.tensor_copy(old[1][:], store[1][:].indirect(slot_sb[:]))
+        for i in range(len(cut3) - 1):
+            nc.scalar.copy(row3_bf[:, cut3[i]:cut3[i + 1]], row3[i][:])
+        for i in range(len(PIECES)):
+            nc.scalar.activation(picked[i][:, :, 3], row3_bf[:].indirect(part[i]), COPY)
 
-        for h in range(2):
-            nc.vector.quantize_mx(out=x_codes[h][:].bitcast(FP8X4), scales=x_scale[h][:], in_=picked[h][:].rearrange("p s j -> p (s j)"))
+        def quantise(i):
+            nc.vector.quantize_mx(out=x_codes[i][:].bitcast(FP8X4), scales=x_scale[i][:], in_=picked[i][:].rearrange("p s j -> p (s j)"))
+
+        for i in range(len(PIECES)):
+            quantise(i)
+        nc.vector.tensor_copy(old[1][:], store[1][:].indirect(slot_sb[:]))
         acc = {}
-        for h in range(2):
+        for i in range(len(PIECES)):
             for b in range(2):
-                acc[b, h] = psum.tile([P, SH], F32, name=f"acc{b}{h}")
-                nc.tensor.matmul_mx(out=acc[b, h][:], lhsT=w_codes[:, b * P:(b + 1) * P].bitcast(FP8X4), lhsT_scale=w_scale[:, b * P:(b + 1) * P],
-                                    rhs=x_codes[h][:].bitcast(FP8X4), rhs_scale=x_scale[h][:], start=True, stop=True)
-        for h in range(2):
+                acc[b, i] = psum.tile([P, PIECES[i]], F32, name=f"acc{b}{i}")
+                nc.tensor.matmul_mx(out=acc[b, i][:], lhsT=w_codes[:, b * P:(b + 1) * P].bitcast(FP8X4), lhsT_scale=w_scale[:, b * P:(b + 1) * P],
+                                    rhs=x_codes[i][:].bitcast(FP8X4), rhs_scale=x_scale[i][:], start=True, stop=True)
+        for i in range(len(PIECES)):
             for b in range(2):
-                cols = slice(h * SH, (h + 1) * SH)
-                nc.vector.tensor_tensor(new[b][:, cols], acc[b, h][:], old[b][:, cols], MAX)
+                cols = slice(starts[i], starts[i + 1])
+                nc.vector.tensor_tensor(new[b][:, cols], acc[b, i][:], old[b][:, cols], MAX)
         for b in range(2):
             nc.vector.tensor_copy(store[b][:].indirect(slot_sb[:]), new[b][:])
             nc.sync.dma_start(out[b * P:(b + 1) * P, :], store[b][:])

@@ -19,8 +19,7 @@ MAX = mybir.AluOpType.max
 
 def tile_picked_idxput_max_e_kernel(tc, xT, mem, w1_words, w1_scales, offs, slot, out):
     nc = tc.nc
-    PIECES = [512]
-    starts = [sum(PIECES[:i]) for i in range(len(PIECES) + 1)]
+    ON_SCALAR = 384
     cut01 = [0,640,1024]
     cut3 = [0,512,1024]
     with ExitStack() as ctx:
@@ -32,15 +31,15 @@ def tile_picked_idxput_max_e_kernel(tc, xT, mem, w1_words, w1_scales, offs, slot
         w_codes = keep.tile([P, N], U32, name="w_codes", align_bytes=64)
         w_scale = keep.tile([P, N], U8, name="w_scale", align_bytes=64)
         row2 = keep.tile([P, T], F32, name="row2")
-        row3 = [keep.tile([P, cut3[i + 1] - cut3[i]], F32, name=f"row3_{i}") for i in range(len(cut3) - 1)]
+        row3 = keep.tile([P, T], F32, name="row3")
         rows01 = [keep.tile([P, 2, cut01[i + 1] - cut01[i]], F32, name=f"rows01_{i}") for i in range(len(cut01) - 1)]
         store = [keep.tile([P, U], F32, name=f"store{b}") for b in range(2)]
         pair = keep.tile([P, T, 2], BF16, name="pair")
         row2_bf = keep.tile([P, T], BF16, name="row2_bf")
         row3_bf = keep.tile([P, T], BF16, name="row3_bf")
-        picked = [keep.tile([P, n, 4], BF16, name=f"picked{i}", align_bytes=64) for i, n in enumerate(PIECES)]
-        x_codes = [keep.tile([P, n], U32, name=f"x_codes{i}", align_bytes=64) for i, n in enumerate(PIECES)]
-        x_scale = [keep.tile([P, n], U8, name=f"x_scale{i}", align_bytes=64) for i, n in enumerate(PIECES)]
+        picked = keep.tile([P, S, 4], BF16, name="picked", align_bytes=64)
+        x_codes = keep.tile([P, S], U32, name="x_codes", align_bytes=64)
+        x_scale = keep.tile([P, S], U8, name="x_scale", align_bytes=64)
         old = [keep.tile([P, S], F32, name=f"old{b}") for b in range(2)]
         new = [keep.tile([P, S], F32, name=f"new{b}") for b in range(2)]
 
@@ -52,49 +51,40 @@ def tile_picked_idxput_max_e_kernel(tc, xT, mem, w1_words, w1_scales, offs, slot
         nc.sync.dma_start(rows01[0][:], xv[:, 0:2, cut01[0]:cut01[1]])
         nc.sync.dma_start(rows01[1][:], xv[:, 0:2, cut01[1]:cut01[2]])
         nc.sync.dma_start(slot_sb[:], slot)
-        nc.sync.dma_start(row3[0][:], xv[:, 3, cut3[0]:cut3[1]])
-        nc.sync.dma_start(row3[1][:], xv[:, 3, cut3[1]:cut3[2]])
+        nc.sync.dma_start(row3[:, cut3[0]:cut3[1]], xv[:, 3, cut3[0]:cut3[1]])
+        nc.sync.dma_start(row3[:, cut3[1]:cut3[2]], xv[:, 3, cut3[1]:cut3[2]])
         nc.sync.dma_start(store[0][:], mem[0 * P:1 * P, :])
         nc.sync.dma_start(store[1][:], mem[1 * P:2 * P, :])
         nc.sync.dma_start(w_codes[:].bitcast(I32), w1_words[0].rearrange("p n t -> p (n t)").bitcast(I32))
         for q in range(4):
             nc.sync.dma_start(w_scale[32 * q:32 * q + 4, :].bitcast(I32), w1_scales[0, 4 * q:4 * q + 4, :].bitcast(I32))
 
-        part = [offs_sb[:, starts[i] // 16:starts[i + 1] // 16] for i in range(len(PIECES))]
+        first = offs_sb[:, 0:ON_SCALAR // 16]
+        rest = offs_sb[:, ON_SCALAR // 16:S // 16]
         nc.scalar.copy(row2_bf[:, 0:320], row2[:, 0:320])
         nc.vector.tensor_copy(row2_bf[:, 320:T], row2[:, 320:T])
-        for i in range(len(PIECES)):
-            nc.scalar.activation(picked[i][:, :, 2], row2_bf[:].indirect(part[i]), COPY)
+        nc.scalar.activation(picked[:, 0:ON_SCALAR, 2], row2_bf[:].indirect(first), COPY)
+        nc.vector.tensor_copy(picked[:, ON_SCALAR:S, 2], row2[:].indirect(rest))
         nc.vector.tensor_copy(pair[:, 0:cut01[1], :], rows01[0][:].rearrange("p j t -> p t j"))
         tail = rows01[1][:].rearrange("p j t -> p t j")
         nc.vector.tensor_copy(pair[:, cut01[1]:T - 128, :], tail[:, 0:T - 128 - cut01[1], :])
         nc.scalar.copy(pair[:, T - 128:T, :], tail[:, T - 128 - cut01[1]:T - cut01[1], :])
         pair_words = pair[:].rearrange("p t j -> p (t j)").bitcast(U32)
-        for i in range(len(PIECES)):
-            picked_words = picked[i][:].rearrange("p s j -> p (s j)").bitcast(U32).rearrange("p (s u) -> p s u", u=2)
-            nc.vector.tensor_copy(picked_words[:, :, 0], pair_words.indirect(part[i]))
-        nc.vector.tensor_copy(old[0][:], store[0][:].indirect(slot_sb[:]))
+        picked_words = picked[:].rearrange("p s j -> p (s j)").bitcast(U32).rearrange("p (s u) -> p s u", u=2)
+        nc.vector.tensor_copy(picked_words[:, :, 0], pair_words.indirect(offs_sb[:]))
         for i in range(len(cut3) - 1):
-            nc.scalar.copy(row3_bf[:, cut3[i]:cut3[i + 1]], row3[i][:])
-        for i in range(len(PIECES)):
-            nc.scalar.activation(picked[i][:, :, 3], row3_bf[:].indirect(part[i]), COPY)
-
-        def quantise(i):
-            nc.vector.quantize_mx(out=x_codes[i][:].bitcast(FP8X4), scales=x_scale[i][:], in_=picked[i][:].rearrange("p s j -> p (s j)"))
-
-        for i in range(len(PIECES)):
-            quantise(i)
+            nc.scalar.copy(row3_bf[:, cut3[i]:cut3[i + 1]], row3[:, cut3[i]:cut3[i + 1]])
+        nc.scalar.activation(picked[:, 0:ON_SCALAR, 3], row3_bf[:].indirect(first), COPY)
+        nc.vector.tensor_copy(picked[:, ON_SCALAR:S, 3], row3[:].indirect(rest))
+        nc.vector.tensor_copy(old[0][:], store[0][:].indirect(slot_sb[:]))
+        nc.vector.quantize_mx(out=x_codes[:].bitcast(FP8X4), scales=x_scale[:], in_=picked[:].rearrange("p s j -> p (s j)"))
         nc.vector.tensor_copy(old[1][:], store[1][:].indirect(slot_sb[:]))
-        acc = {}
-        for i in range(len(PIECES)):
-            for b in range(2):
-                acc[b, i] = psum.tile([P, PIECES[i]], F32, name=f"acc{b}{i}")
-                nc.tensor.matmul_mx(out=acc[b, i][:], lhsT=w_codes[:, b * P:(b + 1) * P].bitcast(FP8X4), lhsT_scale=w_scale[:, b * P:(b + 1) * P],
-                                    rhs=x_codes[i][:].bitcast(FP8X4), rhs_scale=x_scale[i][:], start=True, stop=True)
-        for i in range(len(PIECES)):
-            for b in range(2):
-                cols = slice(starts[i], starts[i + 1])
-                nc.vector.tensor_tensor(new[b][:, cols], acc[b, i][:], old[b][:, cols], MAX)
+        acc = [psum.tile([P, S], F32, name=f"acc{b}") for b in range(2)]
+        for b in range(2):
+            nc.tensor.matmul_mx(out=acc[b][:], lhsT=w_codes[:, b * P:(b + 1) * P].bitcast(FP8X4), lhsT_scale=w_scale[:, b * P:(b + 1) * P],
+                                rhs=x_codes[:].bitcast(FP8X4), rhs_scale=x_scale[:], start=True, stop=True)
+        for b in range(2):
+            nc.vector.tensor_tensor(new[b][:], acc[b][:], old[b][:], MAX)
         for b in range(2):
             nc.vector.tensor_copy(store[b][:].indirect(slot_sb[:]), new[b][:])
             nc.sync.dma_start(out[b * P:(b + 1) * P, :], store[b][:])

@@ -54,10 +54,10 @@ def tile_picked_idxput_max_e_kernel(tc, xT, mem, w1_words, w1_scales, offs, slot
         nc.sync.dma_start(row3[:, cut3[0]:cut3[1]], xv[:, 3, cut3[0]:cut3[1]])
         nc.sync.dma_start(row3[:, cut3[1]:cut3[2]], xv[:, 3, cut3[1]:cut3[2]])
         nc.sync.dma_start(store[0][:], mem[0 * P:1 * P, :])
-        nc.sync.dma_start(store[1][:], mem[1 * P:2 * P, :])
-        nc.sync.dma_start(w_codes[:].bitcast(I32), w1_words[0].rearrange("p n t -> p (n t)").bitcast(I32))
         for q in range(4):
             nc.sync.dma_start(w_scale[32 * q:32 * q + 4, :].bitcast(I32), w1_scales[0, 4 * q:4 * q + 4, :].bitcast(I32))
+        nc.sync.dma_start(store[1][:], mem[1 * P:2 * P, :])
+        nc.sync.dma_start(w_codes[:].bitcast(I32), w1_words[0].rearrange("p n t -> p (n t)").bitcast(I32))
 
         first = offs_sb[:, 0:ON_SCALAR // 16]
         rest = offs_sb[:, ON_SCALAR // 16:S // 16]

@@ -19,9 +19,8 @@ MAX = mybir.AluOpType.max
 
 def tile_picked_idxput_max_e_kernel(tc, xT, mem, w1_words, w1_scales, offs, slot, out):
     nc = tc.nc
-    ON_SCALAR = 384
-    cut01 = [0,640,1024]
-    cut3 = [0,512,1024]
+    A = 128
+    CUT = 768
     with ExitStack() as ctx:
         keep = ctx.enter_context(tc.tile_pool(name="keep", bufs=1))
         psum = ctx.enter_context(tc.psum_pool(name="psum", bufs=1))
@@ -30,61 +29,84 @@ def tile_picked_idxput_max_e_kernel(tc, xT, mem, w1_words, w1_scales, offs, slot
         slot_sb = keep.tile([P, S // 16], U16, name="slot_sb")
         w_codes = keep.tile([P, N], U32, name="w_codes", align_bytes=64)
         w_scale = keep.tile([P, N], U8, name="w_scale", align_bytes=64)
-        row2 = keep.tile([P, T], F32, name="row2")
+        row2w = keep.tile([P, T], F32, name="row2w")
         row3 = keep.tile([P, T], F32, name="row3")
-        rows01 = [keep.tile([P, 2, cut01[i + 1] - cut01[i]], F32, name=f"rows01_{i}") for i in range(len(cut01) - 1)]
+        rows01 = [keep.tile([P, 2, w], F32, name=f"rows01_{i}") for i, w in enumerate((CUT, T - CUT))]
         store = [keep.tile([P, U], F32, name=f"store{b}") for b in range(2)]
         pair = keep.tile([P, T, 2], BF16, name="pair")
         row2_bf = keep.tile([P, T], BF16, name="row2_bf")
         row3_bf = keep.tile([P, T], BF16, name="row3_bf")
         picked = keep.tile([P, S, 4], BF16, name="picked", align_bytes=64)
-        x_codes = keep.tile([P, S], U32, name="x_codes", align_bytes=64)
         x_scale = keep.tile([P, S], U8, name="x_scale", align_bytes=64)
         old = [keep.tile([P, S], F32, name=f"old{b}") for b in range(2)]
         new = [keep.tile([P, S], F32, name=f"new{b}") for b in range(2)]
+        acc = [psum.tile([P, S], F32, name=f"acc{b}") for b in range(2)]
 
         nc.vector.memset(w_scale[:].bitcast(I32), 0)
 
         xv = xT.rearrange("(p j) t -> p j t", j=4)
-        nc.sync.dma_start(row2[:], xv[:, 2, :])
+        nc.sync.dma_start(rows01[0][:], xv[:, 0:2, 0:CUT])
+        nc.sync.dma_start(rows01[1][:], xv[:, 0:2, CUT:T])
         nc.sync.dma_start(offs_sb[:], offs)
-        nc.sync.dma_start(rows01[0][:], xv[:, 0:2, cut01[0]:cut01[1]])
-        nc.sync.dma_start(rows01[1][:], xv[:, 0:2, cut01[1]:cut01[2]])
+        nc.sync.dma_start(row2w[:, 0:T // 2], xv[:, 2, 0:T // 2])
+        nc.sync.dma_start(row2w[:, T // 2:T], xv[:, 2, T // 2:T])
+        nc.sync.dma_start(row3[:], xv[:, 3, :])
         nc.sync.dma_start(slot_sb[:], slot)
-        nc.sync.dma_start(row3[:, cut3[0]:cut3[1]], xv[:, 3, cut3[0]:cut3[1]])
-        nc.sync.dma_start(row3[:, cut3[1]:cut3[2]], xv[:, 3, cut3[1]:cut3[2]])
         nc.sync.dma_start(store[0][:], mem[0 * P:1 * P, :])
         for q in range(4):
             nc.sync.dma_start(w_scale[32 * q:32 * q + 4, :].bitcast(I32), w1_scales[0, 4 * q:4 * q + 4, :].bitcast(I32))
         nc.sync.dma_start(store[1][:], mem[1 * P:2 * P, :])
         nc.sync.dma_start(w_codes[:].bitcast(I32), w1_words[0].rearrange("p n t -> p (n t)").bitcast(I32))
 
-        first = offs_sb[:, 0:ON_SCALAR // 16]
-        rest = offs_sb[:, ON_SCALAR // 16:S // 16]
-        nc.scalar.copy(row2_bf[:, 0:320], row2[:, 0:320])
-        nc.vector.tensor_copy(row2_bf[:, 320:T], row2[:, 320:T])
-        nc.scalar.activation(picked[:, 0:ON_SCALAR, 2], row2_bf[:].indirect(first), COPY)
-        nc.vector.tensor_copy(picked[:, ON_SCALAR:S, 2], row2[:].indirect(rest))
-        nc.vector.tensor_copy(pair[:, 0:cut01[1], :], rows01[0][:].rearrange("p j t -> p t j"))
+        def entries(tile, lo, hi):
+            return tile[:, lo // 16:hi // 16]
+
+        head = rows01[0][:].rearrange("p j t -> p t j")
         tail = rows01[1][:].rearrange("p j t -> p t j")
-        nc.vector.tensor_copy(pair[:, cut01[1]:T - 128, :], tail[:, 0:T - 128 - cut01[1], :])
-        nc.scalar.copy(pair[:, T - 128:T, :], tail[:, T - 128 - cut01[1]:T - cut01[1], :])
+        nc.scalar.copy(pair[:, 0:256, :], head[:, 0:256, :])
+        nc.vector.tensor_copy(pair[:, 256:CUT, :], head[:, 256:CUT, :])
+        nc.scalar.copy(pair[:, CUT:CUT + 80, :], tail[:, 0:80, :])
+        nc.vector.tensor_copy(pair[:, CUT + 80:T, :], tail[:, 80:T - CUT, :])
         pair_words = pair[:].rearrange("p t j -> p (t j)").bitcast(U32)
         picked_words = picked[:].rearrange("p s j -> p (s j)").bitcast(U32).rearrange("p (s u) -> p s u", u=2)
         nc.vector.tensor_copy(picked_words[:, :, 0], pair_words.indirect(offs_sb[:]))
-        for i in range(len(cut3) - 1):
-            nc.scalar.copy(row3_bf[:, cut3[i]:cut3[i + 1]], row3[:, cut3[i]:cut3[i + 1]])
-        nc.scalar.activation(picked[:, 0:ON_SCALAR, 3], row3_bf[:].indirect(first), COPY)
-        nc.vector.tensor_copy(picked[:, ON_SCALAR:S, 3], row3[:].indirect(rest))
-        nc.vector.tensor_copy(old[0][:], store[0][:].indirect(slot_sb[:]))
-        nc.vector.quantize_mx(out=x_codes[:].bitcast(FP8X4), scales=x_scale[:], in_=picked[:].rearrange("p s j -> p (s j)"))
-        nc.vector.tensor_copy(old[1][:], store[1][:].indirect(slot_sb[:]))
-        acc = [psum.tile([P, S], F32, name=f"acc{b}") for b in range(2)]
+        for i in range(2):
+            nc.scalar.copy(row2_bf[:, i * T // 2:(i + 1) * T // 2], row2w[:, i * T // 2:(i + 1) * T // 2])
+        nc.vector.tensor_copy(picked[:, 0:A, 2], row2w[:].indirect(entries(offs_sb, 0, A)))
+        nc.scalar.activation(picked[:, A:S, 2], row2_bf[:].indirect(entries(offs_sb, A, S)), COPY)
+        nc.vector.tensor_copy(picked[:, 0:A, 3], row3[:].indirect(entries(offs_sb, 0, A)))
+        nc.vector.tensor_copy(row3_bf[:, 0:512], row3[:, 0:512])
+        nc.scalar.copy(row3_bf[:, 512:T], row3[:, 512:T])
+        nc.scalar.activation(picked[:, A:S, 3], row3_bf[:].indirect(entries(offs_sb, A, S)), COPY)
+
+        def quantise(codes, base, lo, hi):
+            nc.vector.quantize_mx(out=codes[:, lo - base:hi - base].bitcast(FP8X4), scales=x_scale[:, lo:hi],
+                                  in_=picked[:, lo:hi, :].rearrange("p s j -> p (s j)"))
+
+        def product(b, codes, base, lo, hi):
+            nc.tensor.matmul_mx(out=acc[b][:, lo:hi], lhsT=w_codes[:, b * P:(b + 1) * P].bitcast(FP8X4),
+                                lhsT_scale=w_scale[:, b * P:(b + 1) * P],
+                                rhs=codes[:, lo - base:hi - base].bitcast(FP8X4), rhs_scale=x_scale[:, lo:hi],
+                                start=True, stop=True)
+
+        codes_a = keep.tile([P, A], U32, name="codes_a", tag="codes", align_bytes=64)
+        quantise(codes_a, 0, 0, A)
         for b in range(2):
-            nc.tensor.matmul_mx(out=acc[b][:], lhsT=w_codes[:, b * P:(b + 1) * P].bitcast(FP8X4), lhsT_scale=w_scale[:, b * P:(b + 1) * P],
-                                rhs=x_codes[:].bitcast(FP8X4), rhs_scale=x_scale[:], start=True, stop=True)
+            nc.vector.tensor_copy(old[b][:], store[b][:].indirect(slot_sb[:]))
         for b in range(2):
-            nc.vector.tensor_tensor(new[b][:], acc[b][:], old[b][:], MAX)
+            product(b, codes_a, 0, 0, A)
+        nc.vector.tensor_tensor(new[0][:, 0:A], acc[0][:, 0:A], old[0][:, 0:A], MAX)
+        codes_b = keep.tile([P, S - A], U32, name="codes_b", tag="codes", align_bytes=64)
+        pieces = ((A, 2 * A), (2 * A, S))
+        for lo, hi in pieces:
+            quantise(codes_b, A, lo, hi)
         for b in range(2):
-            nc.vector.tensor_copy(store[b][:].indirect(slot_sb[:]), new[b][:])
-            nc.sync.dma_start(out[b * P:(b + 1) * P, :], store[b][:])
+            for lo, hi in pieces:
+                product(b, codes_b, A, lo, hi)
+        nc.vector.tensor_copy(store[0][:].indirect(entries(slot_sb, 0, A)), new[0][:, 0:A])
+        nc.vector.tensor_tensor(new[0][:, A:S], acc[0][:, A:S], old[0][:, A:S], MAX)
+        nc.vector.tensor_tensor(new[1][:], acc[1][:], old[1][:], MAX)
+        nc.vector.tensor_copy(store[0][:].indirect(entries(slot_sb, A, S)), new[0][:, A:S])
+        nc.sync.dma_start(out[0:P, :], store[0][:])
+        nc.vector.tensor_copy(store[1][:].indirect(slot_sb[:]), new[1][:])
+        nc.sync.dma_start(out[P:2 * P, :], store[1][:])

@@ -20,7 +20,7 @@ MAX = mybir.AluOpType.max
 def tile_picked_idxput_max_e_kernel(tc, xT, mem, w1_words, w1_scales, offs, slot, out):
     nc = tc.nc
     A = 128
-    CUT = 768
+    CUT = 640
     with ExitStack() as ctx:
         keep = ctx.enter_context(tc.tile_pool(name="keep", bufs=1))
         psum = ctx.enter_context(tc.psum_pool(name="psum", bufs=1))
@@ -53,9 +53,9 @@ def tile_picked_idxput_max_e_kernel(tc, xT, mem, w1_words, w1_scales, offs, slot
         nc.sync.dma_start(row3[:], xv[:, 3, :])
         nc.sync.dma_start(slot_sb[:], slot)
         nc.sync.dma_start(store[0][:], mem[0 * P:1 * P, :])
+        nc.sync.dma_start(store[1][:], mem[1 * P:2 * P, :])
         for q in range(4):
             nc.sync.dma_start(w_scale[32 * q:32 * q + 4, :].bitcast(I32), w1_scales[0, 4 * q:4 * q + 4, :].bitcast(I32))
-        nc.sync.dma_start(store[1][:], mem[1 * P:2 * P, :])
         nc.sync.dma_start(w_codes[:].bitcast(I32), w1_words[0].rearrange("p n t -> p (n t)").bitcast(I32))
 
         def entries(tile, lo, hi):
@@ -63,10 +63,10 @@ def tile_picked_idxput_max_e_kernel(tc, xT, mem, w1_words, w1_scales, offs, slot
 
         head = rows01[0][:].rearrange("p j t -> p t j")
         tail = rows01[1][:].rearrange("p j t -> p t j")
-        nc.scalar.copy(pair[:, 0:256, :], head[:, 0:256, :])
-        nc.vector.tensor_copy(pair[:, 256:CUT, :], head[:, 256:CUT, :])
-        nc.scalar.copy(pair[:, CUT:CUT + 80, :], tail[:, 0:80, :])
-        nc.vector.tensor_copy(pair[:, CUT + 80:T, :], tail[:, 80:T - CUT, :])
+        nc.scalar.copy(pair[:, 0:192, :], head[:, 0:192, :])
+        nc.vector.tensor_copy(pair[:, 192:CUT, :], head[:, 192:CUT, :])
+        nc.scalar.copy(pair[:, CUT:CUT + 128, :], tail[:, 0:128, :])
+        nc.vector.tensor_copy(pair[:, CUT + 128:T, :], tail[:, 128:T - CUT, :])
         pair_words = pair[:].rearrange("p t j -> p (t j)").bitcast(U32)
         picked_words = picked[:].rearrange("p s j -> p (s j)").bitcast(U32).rearrange("p (s u) -> p s u", u=2)
         nc.vector.tensor_copy(picked_words[:, :, 0], pair_words.indirect(offs_sb[:]))
@@ -75,8 +75,8 @@ def tile_picked_idxput_max_e_kernel(tc, xT, mem, w1_words, w1_scales, offs, slot
         nc.vector.tensor_copy(picked[:, 0:A, 2], row2w[:].indirect(entries(offs_sb, 0, A)))
         nc.scalar.activation(picked[:, A:S, 2], row2_bf[:].indirect(entries(offs_sb, A, S)), COPY)
         nc.vector.tensor_copy(picked[:, 0:A, 3], row3[:].indirect(entries(offs_sb, 0, A)))
-        nc.vector.tensor_copy(row3_bf[:, 0:512], row3[:, 0:512])
-        nc.scalar.copy(row3_bf[:, 512:T], row3[:, 512:T])
+        nc.vector.tensor_copy(row3_bf[:, 0:256], row3[:, 0:256])
+        nc.scalar.copy(row3_bf[:, 256:T], row3[:, 256:T])
         nc.scalar.activation(picked[:, A:S, 3], row3_bf[:].indirect(entries(offs_sb, A, S)), COPY)
 
         def quantise(codes, base, lo, hi):
@@ -100,8 +100,8 @@ def tile_picked_idxput_max_e_kernel(tc, xT, mem, w1_words, w1_scales, offs, slot
         pieces = ((A, 2 * A), (2 * A, S))
         for lo, hi in pieces:
             quantise(codes_b, A, lo, hi)
-        for b in range(2):
-            for lo, hi in pieces:
+        for lo, hi in pieces:
+            for b in range(2):
                 product(b, codes_b, A, lo, hi)
         nc.vector.tensor_copy(store[0][:].indirect(entries(slot_sb, 0, A)), new[0][:, 0:A])
         nc.vector.tensor_tensor(new[0][:, A:S], acc[0][:, A:S], old[0][:, A:S], MAX)

@@ -75,9 +75,10 @@ def tile_picked_idxput_max_e_kernel(tc, xT, mem, w1_words, w1_scales, offs, slot
         nc.vector.tensor_copy(picked[:, 0:A, 2], row2w[:].indirect(entries(offs_sb, 0, A)))
         nc.scalar.activation(picked[:, A:S, 2], row2_bf[:].indirect(entries(offs_sb, A, S)), COPY)
         nc.vector.tensor_copy(picked[:, 0:A, 3], row3[:].indirect(entries(offs_sb, 0, A)))
-        nc.vector.tensor_copy(row3_bf[:, 0:256], row3[:, 0:256])
-        nc.scalar.copy(row3_bf[:, 256:T], row3[:, 256:T])
-        nc.scalar.activation(picked[:, A:S, 3], row3_bf[:].indirect(entries(offs_sb, A, S)), COPY)
+        nc.vector.tensor_copy(row3_bf[:, 0:448], row3[:, 0:448])
+        nc.scalar.copy(row3_bf[:, 448:T], row3[:, 448:T])
+        for lo, hi in ((A, 2 * A), (2 * A, S)):
+            nc.scalar.activation(picked[:, lo:hi, 3], row3_bf[:].indirect(entries(offs_sb, lo, hi)), COPY)
 
         def quantise(codes, base, lo, hi):
             nc.vector.quantize_mx(out=codes[:, lo - base:hi - base].bitcast(FP8X4), scales=x_scale[:, lo:hi],

@@ -19,8 +19,10 @@ MAX = mybir.AluOpType.max
 
 def tile_picked_idxput_max_e_kernel(tc, xT, mem, w1_words, w1_scales, offs, slot, out):
     nc = tc.nc
-    A = 128
-    CUT = 640
+    DIRECT = 128
+    MID = 384
+    HEAD = 128
+    HALF = S // 2
     with ExitStack() as ctx:
         keep = ctx.enter_context(tc.tile_pool(name="keep", bufs=1))
         psum = ctx.enter_context(tc.psum_pool(name="psum", bufs=1))
@@ -29,85 +31,90 @@ def tile_picked_idxput_max_e_kernel(tc, xT, mem, w1_words, w1_scales, offs, slot
         slot_sb = keep.tile([P, S // 16], U16, name="slot_sb")
         w_codes = keep.tile([P, N], U32, name="w_codes", align_bytes=64)
         w_scale = keep.tile([P, N], U8, name="w_scale", align_bytes=64)
-        row2w = keep.tile([P, T], F32, name="row2w")
-        row3 = keep.tile([P, T], F32, name="row3")
-        rows01 = [keep.tile([P, 2, w], F32, name=f"rows01_{i}") for i, w in enumerate((CUT, T - CUT))]
+        row = [keep.tile([P, T], F32, name=f"row{j}") for j in range(4)]
         store = [keep.tile([P, U], F32, name=f"store{b}") for b in range(2)]
-        pair = keep.tile([P, T, 2], BF16, name="pair")
-        row2_bf = keep.tile([P, T], BF16, name="row2_bf")
-        row3_bf = keep.tile([P, T], BF16, name="row3_bf")
+        flat01 = keep.tile([P, 2, S], BF16, name="flat01")
+        flat23_mid = keep.tile([P, 2, MID - DIRECT], BF16, name="flat23_mid")
+        flat23_end = keep.tile([P, 2, S - MID], BF16, name="flat23_end")
         picked = keep.tile([P, S, 4], BF16, name="picked", align_bytes=64)
+        x_codes = keep.tile([P, S], U32, name="x_codes", align_bytes=64)
         x_scale = keep.tile([P, S], U8, name="x_scale", align_bytes=64)
-        old = [keep.tile([P, S], F32, name=f"old{b}") for b in range(2)]
-        new = [keep.tile([P, S], F32, name=f"new{b}") for b in range(2)]
-        acc = [psum.tile([P, S], F32, name=f"acc{b}") for b in range(2)]
+        acc0_head = psum.tile([P, HEAD], F32, name="acc0_head")
+        acc0_rest = psum.tile([P, S - HEAD], F32, name="acc0_rest")
+        acc1 = psum.tile([P, S], F32, name="acc1")
 
-        nc.vector.memset(w_scale[:].bitcast(I32), 0)
+        warm = keep.tile([P, 2], F32, name="warm")
+        nc.vector.memset(warm[:, 0:1], 0.0)
+        nc.scalar.activation(warm[:, 1:2], warm[:, 0:1], COPY)
 
         xv = xT.rearrange("(p j) t -> p j t", j=4)
-        nc.sync.dma_start(rows01[0][:], xv[:, 0:2, 0:CUT])
-        nc.sync.dma_start(rows01[1][:], xv[:, 0:2, CUT:T])
+        nc.sync.dma_start(row[0][:], xv[:, 0, :])
         nc.sync.dma_start(offs_sb[:], offs)
-        nc.sync.dma_start(row2w[:, 0:T // 2], xv[:, 2, 0:T // 2])
-        nc.sync.dma_start(row2w[:, T // 2:T], xv[:, 2, T // 2:T])
-        nc.sync.dma_start(row3[:], xv[:, 3, :])
+        for j in range(1, 4):
+            nc.sync.dma_start(row[j][:], xv[:, j, :])
         nc.sync.dma_start(slot_sb[:], slot)
-        nc.sync.dma_start(store[0][:], mem[0 * P:1 * P, :])
-        nc.sync.dma_start(store[1][:], mem[1 * P:2 * P, :])
         for q in range(4):
             nc.sync.dma_start(w_scale[32 * q:32 * q + 4, :].bitcast(I32), w1_scales[0, 4 * q:4 * q + 4, :].bitcast(I32))
+        nc.sync.dma_start(store[0][:], mem[0 * P:1 * P, :])
         nc.sync.dma_start(w_codes[:].bitcast(I32), w1_words[0].rearrange("p n t -> p (n t)").bitcast(I32))
+        nc.sync.dma_start(store[1][:], mem[1 * P:2 * P, :])
 
         def entries(tile, lo, hi):
             return tile[:, lo // 16:hi // 16]
 
-        head = rows01[0][:].rearrange("p j t -> p t j")
-        tail = rows01[1][:].rearrange("p j t -> p t j")
-        nc.scalar.copy(pair[:, 0:192, :], head[:, 0:192, :])
-        nc.vector.tensor_copy(pair[:, 192:CUT, :], head[:, 192:CUT, :])
-        nc.scalar.copy(pair[:, CUT:CUT + 128, :], tail[:, 0:128, :])
-        nc.vector.tensor_copy(pair[:, CUT + 128:T, :], tail[:, 128:T - CUT, :])
-        pair_words = pair[:].rearrange("p t j -> p (t j)").bitcast(U32)
-        picked_words = picked[:].rearrange("p s j -> p (s j)").bitcast(U32).rearrange("p (s u) -> p s u", u=2)
-        nc.vector.tensor_copy(picked_words[:, :, 0], pair_words.indirect(offs_sb[:]))
-        for i in range(2):
-            nc.scalar.copy(row2_bf[:, i * T // 2:(i + 1) * T // 2], row2w[:, i * T // 2:(i + 1) * T // 2])
-        nc.vector.tensor_copy(picked[:, 0:A, 2], row2w[:].indirect(entries(offs_sb, 0, A)))
-        nc.scalar.activation(picked[:, A:S, 2], row2_bf[:].indirect(entries(offs_sb, A, S)), COPY)
-        nc.vector.tensor_copy(picked[:, 0:A, 3], row3[:].indirect(entries(offs_sb, 0, A)))
-        nc.vector.tensor_copy(row3_bf[:, 0:448], row3[:, 0:448])
-        nc.scalar.copy(row3_bf[:, 448:T], row3[:, 448:T])
-        for lo, hi in ((A, 2 * A), (2 * A, S)):
-            nc.scalar.activation(picked[:, lo:hi, 3], row3_bf[:].indirect(entries(offs_sb, lo, hi)), COPY)
+        def by_offs(j, lo, hi):
+            return row[j][:].indirect(entries(offs_sb, lo, hi))
 
-        def quantise(codes, base, lo, hi):
-            nc.vector.quantize_mx(out=codes[:, lo - base:hi - base].bitcast(FP8X4), scales=x_scale[:, lo:hi],
+        def by_slot(b, lo, hi):
+            return store[b][:].indirect(entries(slot_sb, lo, hi))
+
+        nc.scalar.activation(flat01[:, 0, :], by_offs(0, 0, S), COPY)
+        nc.vector.tensor_copy(flat01[:, 1, 0:HALF], by_offs(1, 0, HALF))
+        nc.scalar.activation(flat01[:, 1, HALF:S], by_offs(1, HALF, S), COPY)
+        nc.vector.tensor_copy(picked[:, :, 0:2], flat01[:].rearrange("p j s -> p s j"))
+        for j in (2, 3):
+            nc.vector.tensor_copy(picked[:, 0:DIRECT, j], by_offs(j, 0, DIRECT))
+            nc.scalar.activation(flat23_mid[:, j - 2, :], by_offs(j, DIRECT, MID), COPY)
+            nc.scalar.activation(flat23_end[:, j - 2, :], by_offs(j, MID, S), COPY)
+        nc.vector.tensor_copy(picked[:, DIRECT:MID, 2:4], flat23_mid[:].rearrange("p j s -> p s j"))
+        nc.scalar.copy(picked[:, MID:S, 2:4], flat23_end[:].rearrange("p j s -> p s j"))
+
+        pieces = ((0, 128), (128, MID), (MID, S))
+        for lo, hi in pieces:
+            nc.vector.quantize_mx(out=x_codes[:, lo:hi].bitcast(FP8X4), scales=x_scale[:, lo:hi],
                                   in_=picked[:, lo:hi, :].rearrange("p s j -> p (s j)"))
 
-        def product(b, codes, base, lo, hi):
-            nc.tensor.matmul_mx(out=acc[b][:, lo:hi], lhsT=w_codes[:, b * P:(b + 1) * P].bitcast(FP8X4),
-                                lhsT_scale=w_scale[:, b * P:(b + 1) * P],
-                                rhs=codes[:, lo - base:hi - base].bitcast(FP8X4), rhs_scale=x_scale[:, lo:hi],
-                                start=True, stop=True)
+        def sums(b, lo, hi):
+            if b == 1:
+                return acc1[:, lo:hi]
+            return acc0_head[:, lo:hi] if hi <= HEAD else acc0_rest[:, lo - HEAD:hi - HEAD]
 
-        codes_a = keep.tile([P, A], U32, name="codes_a", tag="codes", align_bytes=64)
-        quantise(codes_a, 0, 0, A)
         for b in range(2):
-            nc.vector.tensor_copy(old[b][:], store[b][:].indirect(slot_sb[:]))
-        for b in range(2):
-            product(b, codes_a, 0, 0, A)
-        nc.vector.tensor_tensor(new[0][:, 0:A], acc[0][:, 0:A], old[0][:, 0:A], MAX)
-        codes_b = keep.tile([P, S - A], U32, name="codes_b", tag="codes", align_bytes=64)
-        pieces = ((A, 2 * A), (2 * A, S))
-        for lo, hi in pieces:
-            quantise(codes_b, A, lo, hi)
-        for lo, hi in pieces:
-            for b in range(2):
-                product(b, codes_b, A, lo, hi)
-        nc.vector.tensor_copy(store[0][:].indirect(entries(slot_sb, 0, A)), new[0][:, 0:A])
-        nc.vector.tensor_tensor(new[0][:, A:S], acc[0][:, A:S], old[0][:, A:S], MAX)
-        nc.vector.tensor_tensor(new[1][:], acc[1][:], old[1][:], MAX)
-        nc.vector.tensor_copy(store[0][:].indirect(entries(slot_sb, A, S)), new[0][:, A:S])
+            for lo, hi in pieces:
+                nc.tensor.matmul_mx(out=sums(b, lo, hi), lhsT=w_codes[:, b * P:(b + 1) * P].bitcast(FP8X4),
+                                    lhsT_scale=w_scale[:, b * P:(b + 1) * P],
+                                    rhs=x_codes[:, lo:hi].bitcast(FP8X4), rhs_scale=x_scale[:, lo:hi],
+                                    start=True, stop=True)
+
+        old0_head = keep.tile([P, HEAD], F32, name="old0_head")
+        old0_rest = keep.tile([P, S - HEAD], F32, name="old0_rest")
+        new0_head = keep.tile([P, HEAD], F32, name="new0_head")
+        new0_rest = keep.tile([P, S - HEAD], F32, name="new0_rest")
+        nc.vector.tensor_copy(old0_head[:], by_slot(0, 0, HEAD))
+        nc.scalar.activation(old0_rest[:], by_slot(0, HEAD, S), COPY)
+        nc.vector.tensor_tensor(new0_head[:], acc0_head[:], old0_head[:], MAX)
+        nc.vector.tensor_tensor(new0_rest[:], acc0_rest[:], old0_rest[:], MAX)
+        nc.scalar.activation(by_slot(0, 0, HEAD), new0_head[:], COPY)
+        nc.scalar.activation(by_slot(0, HEAD, S), new0_rest[:], COPY)
         nc.sync.dma_start(out[0:P, :], store[0][:])
-        nc.vector.tensor_copy(store[1][:].indirect(slot_sb[:]), new[1][:])
+
+        halves = ((0, HALF), (HALF, S))
+        old1 = [keep.tile([P, HALF], F32, name=f"old1_{h}") for h in range(2)]
+        new1 = [keep.tile([P, HALF], F32, name=f"new1_{h}") for h in range(2)]
+        for h, (lo, hi) in enumerate(halves):
+            nc.vector.tensor_copy(old1[h][:], by_slot(1, lo, hi))
+        for h, (lo, hi) in enumerate(halves):
+            nc.vector.tensor_tensor(new1[h][:], acc1[:, lo:hi], old1[h][:], MAX)
+        for h, (lo, hi) in enumerate(halves):
+            nc.vector.tensor_copy(by_slot(1, lo, hi), new1[h][:])
         nc.sync.dma_start(out[P:2 * P, :], store[1][:])

@@ -19,10 +19,8 @@ MAX = mybir.AluOpType.max
 
 def tile_picked_idxput_max_e_kernel(tc, xT, mem, w1_words, w1_scales, offs, slot, out):
     nc = tc.nc
-    DIRECT = 128
-    MID = 384
-    HEAD = 128
     HALF = S // 2
+    EDGE = S // 4
     with ExitStack() as ctx:
         keep = ctx.enter_context(tc.tile_pool(name="keep", bufs=1))
         psum = ctx.enter_context(tc.psum_pool(name="psum", bufs=1))
@@ -33,19 +31,17 @@ def tile_picked_idxput_max_e_kernel(tc, xT, mem, w1_words, w1_scales, offs, slot
         w_scale = keep.tile([P, N], U8, name="w_scale", align_bytes=64)
         row = [keep.tile([P, T], F32, name=f"row{j}") for j in range(4)]
         store = [keep.tile([P, U], F32, name=f"store{b}") for b in range(2)]
-        flat01 = keep.tile([P, 2, S], BF16, name="flat01")
-        flat23_mid = keep.tile([P, 2, MID - DIRECT], BF16, name="flat23_mid")
-        flat23_end = keep.tile([P, 2, S - MID], BF16, name="flat23_end")
+        flat = [[keep.tile([P, 2, EDGE], BF16, name=f"flat{u}_{e}") for e in range(2)] for u in range(2)]
         picked = keep.tile([P, S, 4], BF16, name="picked", align_bytes=64)
-        x_codes = keep.tile([P, S], U32, name="x_codes", align_bytes=64)
         x_scale = keep.tile([P, S], U8, name="x_scale", align_bytes=64)
-        acc0_head = psum.tile([P, HEAD], F32, name="acc0_head")
-        acc0_rest = psum.tile([P, S - HEAD], F32, name="acc0_rest")
-        acc1 = psum.tile([P, S], F32, name="acc1")
+        acc = [[psum.tile([P, HALF], F32, name=f"acc{b}_{h}") for h in range(2)] for b in range(2)]
 
         warm = keep.tile([P, 2], F32, name="warm")
         nc.vector.memset(warm[:, 0:1], 0.0)
         nc.scalar.activation(warm[:, 1:2], warm[:, 0:1], COPY)
+
+        for q in range(4):
+            nc.scalar.dma_start(w_scale[32 * q:32 * q + 4, :].bitcast(I32), w1_scales[0, 4 * q:4 * q + 4, :].bitcast(I32))
 
         xv = xT.rearrange("(p j) t -> p j t", j=4)
         nc.sync.dma_start(row[0][:], xv[:, 0, :])
@@ -53,8 +49,6 @@ def tile_picked_idxput_max_e_kernel(tc, xT, mem, w1_words, w1_scales, offs, slot
         for j in range(1, 4):
             nc.sync.dma_start(row[j][:], xv[:, j, :])
         nc.sync.dma_start(slot_sb[:], slot)
-        for q in range(4):
-            nc.sync.dma_start(w_scale[32 * q:32 * q + 4, :].bitcast(I32), w1_scales[0, 4 * q:4 * q + 4, :].bitcast(I32))
         nc.sync.dma_start(store[0][:], mem[0 * P:1 * P, :])
         nc.sync.dma_start(w_codes[:].bitcast(I32), w1_words[0].rearrange("p n t -> p (n t)").bitcast(I32))
         nc.sync.dma_start(store[1][:], mem[1 * P:2 * P, :])
@@ -68,53 +62,48 @@ def tile_picked_idxput_max_e_kernel(tc, xT, mem, w1_words, w1_scales, offs, slot
         def by_slot(b, lo, hi):
             return store[b][:].indirect(entries(slot_sb, lo, hi))
 
-        nc.scalar.activation(flat01[:, 0, :], by_offs(0, 0, S), COPY)
-        nc.vector.tensor_copy(flat01[:, 1, 0:HALF], by_offs(1, 0, HALF))
-        nc.scalar.activation(flat01[:, 1, HALF:S], by_offs(1, HALF, S), COPY)
-        nc.vector.tensor_copy(picked[:, :, 0:2], flat01[:].rearrange("p j s -> p s j"))
-        for j in (2, 3):
-            nc.vector.tensor_copy(picked[:, 0:DIRECT, j], by_offs(j, 0, DIRECT))
-            nc.scalar.activation(flat23_mid[:, j - 2, :], by_offs(j, DIRECT, MID), COPY)
-            nc.scalar.activation(flat23_end[:, j - 2, :], by_offs(j, MID, S), COPY)
-        nc.vector.tensor_copy(picked[:, DIRECT:MID, 2:4], flat23_mid[:].rearrange("p j s -> p s j"))
-        nc.scalar.copy(picked[:, MID:S, 2:4], flat23_end[:].rearrange("p j s -> p s j"))
-
-        pieces = ((0, 128), (128, MID), (MID, S))
-        for lo, hi in pieces:
-            nc.vector.quantize_mx(out=x_codes[:, lo:hi].bitcast(FP8X4), scales=x_scale[:, lo:hi],
-                                  in_=picked[:, lo:hi, :].rearrange("p s j -> p (s j)"))
-
-        def sums(b, lo, hi):
-            if b == 1:
-                return acc1[:, lo:hi]
-            return acc0_head[:, lo:hi] if hi <= HEAD else acc0_rest[:, lo - HEAD:hi - HEAD]
-
-        for b in range(2):
-            for lo, hi in pieces:
-                nc.tensor.matmul_mx(out=sums(b, lo, hi), lhsT=w_codes[:, b * P:(b + 1) * P].bitcast(FP8X4),
-                                    lhsT_scale=w_scale[:, b * P:(b + 1) * P],
-                                    rhs=x_codes[:, lo:hi].bitcast(FP8X4), rhs_scale=x_scale[:, lo:hi],
-                                    start=True, stop=True)
-
-        old0_head = keep.tile([P, HEAD], F32, name="old0_head")
-        old0_rest = keep.tile([P, S - HEAD], F32, name="old0_rest")
-        new0_head = keep.tile([P, HEAD], F32, name="new0_head")
-        new0_rest = keep.tile([P, S - HEAD], F32, name="new0_rest")
-        nc.vector.tensor_copy(old0_head[:], by_slot(0, 0, HEAD))
-        nc.scalar.activation(old0_rest[:], by_slot(0, HEAD, S), COPY)
-        nc.vector.tensor_tensor(new0_head[:], acc0_head[:], old0_head[:], MAX)
-        nc.vector.tensor_tensor(new0_rest[:], acc0_rest[:], old0_rest[:], MAX)
-        nc.scalar.activation(by_slot(0, 0, HEAD), new0_head[:], COPY)
-        nc.scalar.activation(by_slot(0, HEAD, S), new0_rest[:], COPY)
-        nc.sync.dma_start(out[0:P, :], store[0][:])
+        edges = ((0, EDGE), (S - EDGE, S))
+        for u in range(2):
+            for i in range(2):
+                j = 2 * u + i
+                nc.vector.tensor_copy(picked[:, EDGE:S - EDGE, j], by_offs(j, EDGE, S - EDGE))
+                for e, (lo, hi) in enumerate(edges):
+                    nc.scalar.activation(flat[u][e][:, i, :], by_offs(j, lo, hi), COPY)
+            for e, (lo, hi) in enumerate(edges):
+                nc.vector.tensor_copy(picked[:, lo:hi, 2 * u:2 * u + 2], flat[u][e][:].rearrange("p j s -> p s j"))
 
         halves = ((0, HALF), (HALF, S))
-        old1 = [keep.tile([P, HALF], F32, name=f"old1_{h}") for h in range(2)]
-        new1 = [keep.tile([P, HALF], F32, name=f"new1_{h}") for h in range(2)]
+        x_codes = [keep.tile([P, HALF], U32, name=f"x_codes{h}", align_bytes=64) for h in range(2)]
         for h, (lo, hi) in enumerate(halves):
-            nc.vector.tensor_copy(old1[h][:], by_slot(1, lo, hi))
+            nc.vector.quantize_mx(out=x_codes[h][:].bitcast(FP8X4), scales=x_scale[:, lo:hi],
+                                  in_=picked[:, lo:hi, :].rearrange("p s j -> p (s j)"))
+
+        def product(b, h):
+            lo, hi = halves[h]
+            nc.tensor.matmul_mx(out=acc[b][h][:], lhsT=w_codes[:, b * P:(b + 1) * P].bitcast(FP8X4),
+                                lhsT_scale=w_scale[:, b * P:(b + 1) * P],
+                                rhs=x_codes[h][:].bitcast(FP8X4), rhs_scale=x_scale[:, lo:hi],
+                                start=True, stop=True)
+
+        for b in range(2):
+            for h in range(2):
+                product(b, h)
+
+        old = [[keep.tile([P, HALF], F32, name=f"old{b}_{h}") for h in range(2)] for b in range(2)]
+        new = [[keep.tile([P, HALF], F32, name=f"new{b}_{h}") for h in range(2)] for b in range(2)]
+        nc.scalar.activation(old[0][0][:], by_slot(0, 0, HALF), COPY)
+        nc.scalar.activation(old[0][1][:, 0:EDGE], by_slot(0, HALF, S - EDGE), COPY)
+        nc.vector.tensor_copy(old[0][1][:, EDGE:HALF], by_slot(0, S - EDGE, S))
+        for h in range(2):
+            nc.vector.tensor_tensor(new[0][h][:], acc[0][h][:], old[0][h][:], MAX)
         for h, (lo, hi) in enumerate(halves):
-            nc.vector.tensor_tensor(new1[h][:], acc1[:, lo:hi], old1[h][:], MAX)
+            nc.scalar.activation(by_slot(0, lo, hi), new[0][h][:], COPY)
+        nc.sync.dma_start(out[0:P, :], store[0][:])
+
         for h, (lo, hi) in enumerate(halves):
-            nc.vector.tensor_copy(by_slot(1, lo, hi), new1[h][:])
+            nc.vector.tensor_copy(old[1][h][:], by_slot(1, lo, hi))
+        for h in range(2):
+            nc.vector.tensor_tensor(new[1][h][:], acc[1][h][:], old[1][h][:], MAX)
+        for h, (lo, hi) in enumerate(halves):
+            nc.vector.tensor_copy(by_slot(1, lo, hi), new[1][h][:])
         nc.sync.dma_start(out[P:2 * P, :], store[1][:])

@@ -27,7 +27,7 @@ def tile_picked_idxput_max_e_kernel(tc, xT, mem, w1_words, w1_scales, offs, slot
 
         offs_sb = keep.tile([P, S // 16], U16, name="offs_sb")
         slot_sb = keep.tile([P, S // 16], U16, name="slot_sb")
-        w_codes = keep.tile([P, N], U32, name="w_codes", align_bytes=64)
+        w_codes = [keep.tile([P, P], U32, name=f"w_codes{b}", align_bytes=64) for b in range(2)]
         w_scale = keep.tile([P, N], U8, name="w_scale", align_bytes=64)
         row = [keep.tile([P, T], F32, name=f"row{j}") for j in range(4)]
         store = [keep.tile([P, U], F32, name=f"store{b}") for b in range(2)]
@@ -49,9 +49,10 @@ def tile_picked_idxput_max_e_kernel(tc, xT, mem, w1_words, w1_scales, offs, slot
         for j in range(1, 4):
             nc.sync.dma_start(row[j][:], xv[:, j, :])
         nc.sync.dma_start(slot_sb[:], slot)
-        nc.sync.dma_start(store[0][:], mem[0 * P:1 * P, :])
-        nc.sync.dma_start(w_codes[:].bitcast(I32), w1_words[0].rearrange("p n t -> p (n t)").bitcast(I32))
-        nc.sync.dma_start(store[1][:], mem[1 * P:2 * P, :])
+        w_words = w1_words[0].rearrange("p n t -> p (n t)").bitcast(I32)
+        for b in range(2):
+            nc.sync.dma_start(store[b][:], mem[b * P:(b + 1) * P, :])
+            nc.sync.dma_start(w_codes[b][:].bitcast(I32), w_words[:, b * P:(b + 1) * P])
 
         def entries(tile, lo, hi):
             return tile[:, lo // 16:hi // 16]
@@ -80,7 +81,7 @@ def tile_picked_idxput_max_e_kernel(tc, xT, mem, w1_words, w1_scales, offs, slot
 
         def product(b, h):
             lo, hi = halves[h]
-            nc.tensor.matmul_mx(out=acc[b][h][:], lhsT=w_codes[:, b * P:(b + 1) * P].bitcast(FP8X4),
+            nc.tensor.matmul_mx(out=acc[b][h][:], lhsT=w_codes[b][:].bitcast(FP8X4),
                                 lhsT_scale=w_scale[:, b * P:(b + 1) * P],
                                 rhs=x_codes[h][:].bitcast(FP8X4), rhs_scale=x_scale[:, lo:hi],
                                 start=True, stop=True)
@@ -89,21 +90,21 @@ def tile_picked_idxput_max_e_kernel(tc, xT, mem, w1_words, w1_scales, offs, slot
             for h in range(2):
                 product(b, h)
 
-        old = [[keep.tile([P, HALF], F32, name=f"old{b}_{h}") for h in range(2)] for b in range(2)]
-        new = [[keep.tile([P, HALF], F32, name=f"new{b}_{h}") for h in range(2)] for b in range(2)]
-        nc.scalar.activation(old[0][0][:], by_slot(0, 0, HALF), COPY)
-        nc.scalar.activation(old[0][1][:, 0:EDGE], by_slot(0, HALF, S - EDGE), COPY)
-        nc.vector.tensor_copy(old[0][1][:, EDGE:HALF], by_slot(0, S - EDGE, S))
-        for h in range(2):
-            nc.vector.tensor_tensor(new[0][h][:], acc[0][h][:], old[0][h][:], MAX)
+        old0 = [keep.tile([P, HALF], F32, name=f"old0_{h}") for h in range(2)]
+        old1 = [keep.tile([P, HALF], F32, name="old1_0", tag="turn"), keep.tile([P, HALF], F32, name="old1_1")]
+        new1 = keep.tile([P, S], F32, name="new1")
+        new0_lo = keep.tile([P, HALF], F32, name="new0_lo")
         for h, (lo, hi) in enumerate(halves):
-            nc.scalar.activation(by_slot(0, lo, hi), new[0][h][:], COPY)
-        nc.sync.dma_start(out[0:P, :], store[0][:])
-
+            nc.scalar.activation(old0[h][:], by_slot(0, lo, hi), COPY)
+        nc.vector.tensor_tensor(new0_lo[:], acc[0][0][:], old0[0][:], MAX)
+        nc.scalar.activation(by_slot(0, 0, HALF), new0_lo[:], COPY)
         for h, (lo, hi) in enumerate(halves):
-            nc.vector.tensor_copy(old[1][h][:], by_slot(1, lo, hi))
-        for h in range(2):
-            nc.vector.tensor_tensor(new[1][h][:], acc[1][h][:], old[1][h][:], MAX)
+            nc.vector.tensor_copy(old1[h][:], by_slot(1, lo, hi))
         for h, (lo, hi) in enumerate(halves):
-            nc.vector.tensor_copy(by_slot(1, lo, hi), new[1][h][:])
+            nc.vector.tensor_tensor(new1[:, lo:hi], acc[1][h][:], old1[h][:], MAX)
+        new0_hi = keep.tile([P, HALF], F32, name="new0_hi", tag="turn")
+        nc.vector.tensor_tensor(new0_hi[:], acc[0][1][:], old0[1][:], MAX)
+        nc.scalar.activation(by_slot(0, HALF, S), new0_hi[:], COPY)
+        nc.scalar.dma_start(out[0:P, :], store[0][:])
+        nc.vector.tensor_copy(by_slot(1, 0, S), new1[:])
         nc.sync.dma_start(out[P:2 * P, :], store[1][:])

@@ -21,6 +21,7 @@ def tile_picked_idxput_max_e_kernel(tc, xT, mem, w1_words, w1_scales, offs, slot
     nc = tc.nc
     HALF = S // 2
     EDGE = S // 4
+    SPARE = 96
     with ExitStack() as ctx:
         keep = ctx.enter_context(tc.tile_pool(name="keep", bufs=1))
         psum = ctx.enter_context(tc.psum_pool(name="psum", bufs=1))
@@ -94,8 +95,9 @@ def tile_picked_idxput_max_e_kernel(tc, xT, mem, w1_words, w1_scales, offs, slot
         old1 = [keep.tile([P, HALF], F32, name="old1_0", tag="turn"), keep.tile([P, HALF], F32, name="old1_1")]
         new1 = keep.tile([P, S], F32, name="new1")
         new0_lo = keep.tile([P, HALF], F32, name="new0_lo")
-        for h, (lo, hi) in enumerate(halves):
-            nc.scalar.activation(old0[h][:], by_slot(0, lo, hi), COPY)
+        nc.scalar.activation(old0[0][:], by_slot(0, 0, HALF), COPY)
+        nc.scalar.activation(old0[1][:, 0:HALF - SPARE], by_slot(0, HALF, S - SPARE), COPY)
+        nc.vector.tensor_copy(old0[1][:, HALF - SPARE:HALF], by_slot(0, S - SPARE, S))
         nc.vector.tensor_tensor(new0_lo[:], acc[0][0][:], old0[0][:], MAX)
         nc.scalar.activation(by_slot(0, 0, HALF), new0_lo[:], COPY)
         for h, (lo, hi) in enumerate(halves):

@@ -21,7 +21,6 @@ def tile_picked_idxput_max_e_kernel(tc, xT, mem, w1_words, w1_scales, offs, slot
     nc = tc.nc
     HALF = S // 2
     EDGE = S // 4
-    SPARE = 96
     with ExitStack() as ctx:
         keep = ctx.enter_context(tc.tile_pool(name="keep", bufs=1))
         psum = ctx.enter_context(tc.psum_pool(name="psum", bufs=1))
@@ -32,10 +31,8 @@ def tile_picked_idxput_max_e_kernel(tc, xT, mem, w1_words, w1_scales, offs, slot
         w_scale = keep.tile([P, N], U8, name="w_scale", align_bytes=64)
         row = [keep.tile([P, T], F32, name=f"row{j}") for j in range(4)]
         store = [keep.tile([P, U], F32, name=f"store{b}") for b in range(2)]
-        flat = [[keep.tile([P, 2, EDGE], BF16, name=f"flat{u}_{e}") for e in range(2)] for u in range(2)]
         picked = keep.tile([P, S, 4], BF16, name="picked", align_bytes=64)
         x_scale = keep.tile([P, S], U8, name="x_scale", align_bytes=64)
-        acc = [[psum.tile([P, HALF], F32, name=f"acc{b}_{h}") for h in range(2)] for b in range(2)]
 
         warm = keep.tile([P, 2], F32, name="warm")
         nc.vector.memset(warm[:, 0:1], 0.0)
@@ -45,15 +42,7 @@ def tile_picked_idxput_max_e_kernel(tc, xT, mem, w1_words, w1_scales, offs, slot
             nc.scalar.dma_start(w_scale[32 * q:32 * q + 4, :].bitcast(I32), w1_scales[0, 4 * q:4 * q + 4, :].bitcast(I32))
 
         xv = xT.rearrange("(p j) t -> p j t", j=4)
-        nc.sync.dma_start(row[0][:], xv[:, 0, :])
-        nc.sync.dma_start(offs_sb[:], offs)
-        for j in range(1, 4):
-            nc.sync.dma_start(row[j][:], xv[:, j, :])
-        nc.sync.dma_start(slot_sb[:], slot)
         w_words = w1_words[0].rearrange("p n t -> p (n t)").bitcast(I32)
-        for b in range(2):
-            nc.sync.dma_start(store[b][:], mem[b * P:(b + 1) * P, :])
-            nc.sync.dma_start(w_codes[b][:].bitcast(I32), w_words[:, b * P:(b + 1) * P])
 
         def entries(tile, lo, hi):
             return tile[:, lo // 16:hi // 16]
@@ -64,7 +53,29 @@ def tile_picked_idxput_max_e_kernel(tc, xT, mem, w1_words, w1_scales, offs, slot
         def by_slot(b, lo, hi):
             return store[b][:].indirect(entries(slot_sb, lo, hi))
 
+        def load_row(j):
+            nc.sync.dma_start(row[j][:], xv[:, j, :])
+
+        def load_band(b, lo=0, hi=U):
+            nc.sync.dma_start(store[b][:, lo:hi], mem[b * P:(b + 1) * P, lo:hi])
+
+        def load_words(b):
+            nc.sync.dma_start(w_codes[b][:].bitcast(I32), w_words[:, b * P:(b + 1) * P])
+
+        load_row(0)
+        nc.sync.dma_start(offs_sb[:], offs)
+        for j in range(1, 4):
+            load_row(j)
+        nc.sync.dma_start(slot_sb[:], slot)
+        load_band(0)
+        load_band(1, 0, 416)
+        load_words(0)
+        load_band(1, 416, U)
+        load_words(1)
+
         edges = ((0, EDGE), (S - EDGE, S))
+        halves = ((0, HALF), (HALF, S))
+        flat = [[keep.tile([P, 2, EDGE], BF16, name=f"flat{u}_{e}") for e in range(2)] for u in range(2)]
         for u in range(2):
             for i in range(2):
                 j = 2 * u + i
@@ -74,39 +85,43 @@ def tile_picked_idxput_max_e_kernel(tc, xT, mem, w1_words, w1_scales, offs, slot
             for e, (lo, hi) in enumerate(edges):
                 nc.vector.tensor_copy(picked[:, lo:hi, 2 * u:2 * u + 2], flat[u][e][:].rearrange("p j s -> p s j"))
 
-        halves = ((0, HALF), (HALF, S))
         x_codes = [keep.tile([P, HALF], U32, name=f"x_codes{h}", align_bytes=64) for h in range(2)]
         for h, (lo, hi) in enumerate(halves):
             nc.vector.quantize_mx(out=x_codes[h][:].bitcast(FP8X4), scales=x_scale[:, lo:hi],
                                   in_=picked[:, lo:hi, :].rearrange("p s j -> p (s j)"))
 
-        def product(b, h):
+        def product(dst, b, h):
             lo, hi = halves[h]
-            nc.tensor.matmul_mx(out=acc[b][h][:], lhsT=w_codes[b][:].bitcast(FP8X4),
+            nc.tensor.matmul_mx(out=dst, lhsT=w_codes[b][:].bitcast(FP8X4),
                                 lhsT_scale=w_scale[:, b * P:(b + 1) * P],
                                 rhs=x_codes[h][:].bitcast(FP8X4), rhs_scale=x_scale[:, lo:hi],
                                 start=True, stop=True)
 
-        for b in range(2):
-            for h in range(2):
-                product(b, h)
+        acc0 = [psum.tile([P, HALF], F32, name=f"acc0_{h}") for h in range(2)]
+        acc1 = psum.tile([P, S], F32, name="acc1")
+        for h in range(2):
+            product(acc0[h][:], 0, h)
+        for h, (lo, hi) in enumerate(halves):
+            product(acc1[:, lo:hi], 1, h)
 
+        V0, V1 = 160, 224
         old0 = [keep.tile([P, HALF], F32, name=f"old0_{h}") for h in range(2)]
-        old1 = [keep.tile([P, HALF], F32, name="old1_0", tag="turn"), keep.tile([P, HALF], F32, name="old1_1")]
+        old1_s = keep.tile([P, S - V1], F32, name="old1_s", tag="turn")
+        old1_v = keep.tile([P, V1], F32, name="old1_v")
         new1 = keep.tile([P, S], F32, name="new1")
         new0_lo = keep.tile([P, HALF], F32, name="new0_lo")
         nc.scalar.activation(old0[0][:], by_slot(0, 0, HALF), COPY)
-        nc.scalar.activation(old0[1][:, 0:HALF - SPARE], by_slot(0, HALF, S - SPARE), COPY)
-        nc.vector.tensor_copy(old0[1][:, HALF - SPARE:HALF], by_slot(0, S - SPARE, S))
-        nc.vector.tensor_tensor(new0_lo[:], acc[0][0][:], old0[0][:], MAX)
+        nc.scalar.activation(old0[1][:, 0:HALF - V0], by_slot(0, HALF, S - V0), COPY)
+        nc.vector.tensor_copy(old0[1][:, HALF - V0:HALF], by_slot(0, S - V0, S))
+        nc.scalar.activation(old1_s[:], by_slot(1, V1, S), COPY)
+        nc.vector.tensor_tensor(new0_lo[:], acc0[0][:], old0[0][:], MAX)
         nc.scalar.activation(by_slot(0, 0, HALF), new0_lo[:], COPY)
-        for h, (lo, hi) in enumerate(halves):
-            nc.vector.tensor_copy(old1[h][:], by_slot(1, lo, hi))
-        for h, (lo, hi) in enumerate(halves):
-            nc.vector.tensor_tensor(new1[:, lo:hi], acc[1][h][:], old1[h][:], MAX)
+        nc.vector.tensor_copy(old1_v[:], by_slot(1, 0, V1))
+        nc.vector.tensor_tensor(new1[:, V1:S], acc1[:, V1:S], old1_s[:], MAX)
+        nc.vector.tensor_tensor(new1[:, 0:V1], acc1[:, 0:V1], old1_v[:], MAX)
         new0_hi = keep.tile([P, HALF], F32, name="new0_hi", tag="turn")
-        nc.vector.tensor_tensor(new0_hi[:], acc[0][1][:], old0[1][:], MAX)
+        nc.vector.tensor_tensor(new0_hi[:], acc0[1][:], old0[1][:], MAX)
         nc.scalar.activation(by_slot(0, HALF, S), new0_hi[:], COPY)
-        nc.scalar.dma_start(out[0:P, :], store[0][:])
+        nc.sync.dma_start(out[0:P, :], store[0][:])
         nc.vector.tensor_copy(by_slot(1, 0, S), new1[:])
-        nc.sync.dma_start(out[P:2 * P, :], store[1][:])
+        nc.scalar.dma_start(out[P:2 * P, :], store[1][:])

@@ -104,7 +104,7 @@ def tile_picked_idxput_max_e_kernel(tc, xT, mem, w1_words, w1_scales, offs, slot
         for h, (lo, hi) in enumerate(halves):
             product(acc1[:, lo:hi], 1, h)
 
-        V0, V1 = 160, 224
+        V0, V1 = 96, 288
         old0 = [keep.tile([P, HALF], F32, name=f"old0_{h}") for h in range(2)]
         old1_s = keep.tile([P, S - V1], F32, name="old1_s", tag="turn")
         old1_v = keep.tile([P, V1], F32, name="old1_v")

@@ -21,6 +21,8 @@ def tile_picked_idxput_max_e_kernel(tc, xT, mem, w1_words, w1_scales, offs, slot
     nc = tc.nc
     HALF = S // 2
     EDGE = S // 4
+    COPIED = 896
+    V1 = 352
     with ExitStack() as ctx:
         keep = ctx.enter_context(tc.tile_pool(name="keep", bufs=1))
         psum = ctx.enter_context(tc.psum_pool(name="psum", bufs=1))
@@ -30,6 +32,7 @@ def tile_picked_idxput_max_e_kernel(tc, xT, mem, w1_words, w1_scales, offs, slot
         w_codes = [keep.tile([P, P], U32, name=f"w_codes{b}", align_bytes=64) for b in range(2)]
         w_scale = keep.tile([P, N], U8, name="w_scale", align_bytes=64)
         row = [keep.tile([P, T], F32, name=f"row{j}") for j in range(4)]
+        table0 = keep.tile([P, U], F32, name="table0")
         store = [keep.tile([P, U], F32, name=f"store{b}") for b in range(2)]
         picked = keep.tile([P, S, 4], BF16, name="picked", align_bytes=64)
         x_scale = keep.tile([P, S], U8, name="x_scale", align_bytes=64)
@@ -44,34 +47,22 @@ def tile_picked_idxput_max_e_kernel(tc, xT, mem, w1_words, w1_scales, offs, slot
         xv = xT.rearrange("(p j) t -> p j t", j=4)
         w_words = w1_words[0].rearrange("p n t -> p (n t)").bitcast(I32)
 
-        def entries(tile, lo, hi):
-            return tile[:, lo // 16:hi // 16]
-
-        def by_offs(j, lo, hi):
-            return row[j][:].indirect(entries(offs_sb, lo, hi))
-
-        def by_slot(b, lo, hi):
-            return store[b][:].indirect(entries(slot_sb, lo, hi))
-
-        def load_row(j):
-            nc.sync.dma_start(row[j][:], xv[:, j, :])
-
-        def load_band(b, lo=0, hi=U):
-            nc.sync.dma_start(store[b][:, lo:hi], mem[b * P:(b + 1) * P, lo:hi])
+        def look_up(window, offsets, lo, hi):
+            return window[:].indirect(offsets[:, lo // 16:hi // 16])
 
         def load_words(b):
             nc.sync.dma_start(w_codes[b][:].bitcast(I32), w_words[:, b * P:(b + 1) * P])
 
-        load_row(0)
+        nc.sync.dma_start(row[0][:], xv[:, 0, :])
         nc.sync.dma_start(offs_sb[:], offs)
         for j in range(1, 4):
-            load_row(j)
+            nc.sync.dma_start(row[j][:], xv[:, j, :])
         nc.sync.dma_start(slot_sb[:], slot)
-        load_band(0)
-        load_band(1, 0, 416)
         load_words(0)
-        load_band(1, 416, U)
+        nc.sync.dma_start(table0[:], mem[0:P, :])
+        nc.sync.dma_start(store[1][:], mem[P:2 * P, :])
         load_words(1)
+        nc.sync.dma_start(store[0][:, COPIED:U], mem[0:P, COPIED:U])
 
         edges = ((0, EDGE), (S - EDGE, S))
         halves = ((0, HALF), (HALF, S))
@@ -79,9 +70,9 @@ def tile_picked_idxput_max_e_kernel(tc, xT, mem, w1_words, w1_scales, offs, slot
         for u in range(2):
             for i in range(2):
                 j = 2 * u + i
-                nc.vector.tensor_copy(picked[:, EDGE:S - EDGE, j], by_offs(j, EDGE, S - EDGE))
+                nc.vector.tensor_copy(picked[:, EDGE:S - EDGE, j], look_up(row[j], offs_sb, EDGE, S - EDGE))
                 for e, (lo, hi) in enumerate(edges):
-                    nc.scalar.activation(flat[u][e][:, i, :], by_offs(j, lo, hi), COPY)
+                    nc.scalar.activation(flat[u][e][:, i, :], look_up(row[j], offs_sb, lo, hi), COPY)
             for e, (lo, hi) in enumerate(edges):
                 nc.vector.tensor_copy(picked[:, lo:hi, 2 * u:2 * u + 2], flat[u][e][:].rearrange("p j s -> p s j"))
 
@@ -98,30 +89,30 @@ def tile_picked_idxput_max_e_kernel(tc, xT, mem, w1_words, w1_scales, offs, slot
                                 start=True, stop=True)
 
         acc0 = [psum.tile([P, HALF], F32, name=f"acc0_{h}") for h in range(2)]
-        acc1 = psum.tile([P, S], F32, name="acc1")
+        acc1 = [psum.tile([P, HALF], F32, name=f"acc1_{h}") for h in range(2)]
         for h in range(2):
             product(acc0[h][:], 0, h)
-        for h, (lo, hi) in enumerate(halves):
-            product(acc1[:, lo:hi], 1, h)
+        for h in (1, 0):
+            product(acc1[h][:], 1, h)
 
-        V0, V1 = 96, 288
         old0 = [keep.tile([P, HALF], F32, name=f"old0_{h}") for h in range(2)]
-        old1_s = keep.tile([P, S - V1], F32, name="old1_s", tag="turn")
-        old1_v = keep.tile([P, V1], F32, name="old1_v")
+        old1_hi = keep.tile([P, HALF], F32, name="old1_hi", tag="turn")
+        old1_lo = keep.tile([P, HALF], F32, name="old1_lo")
         new1 = keep.tile([P, S], F32, name="new1")
         new0_lo = keep.tile([P, HALF], F32, name="new0_lo")
-        nc.scalar.activation(old0[0][:], by_slot(0, 0, HALF), COPY)
-        nc.scalar.activation(old0[1][:, 0:HALF - V0], by_slot(0, HALF, S - V0), COPY)
-        nc.vector.tensor_copy(old0[1][:, HALF - V0:HALF], by_slot(0, S - V0, S))
-        nc.scalar.activation(old1_s[:], by_slot(1, V1, S), COPY)
+        nc.vector.tensor_copy(store[0][:, 0:COPIED], table0[:, 0:COPIED])
+        for h, (lo, hi) in enumerate(halves):
+            nc.scalar.activation(old0[h][:], look_up(table0, slot_sb, lo, hi), COPY)
+        nc.scalar.activation(old1_hi[:, V1 - HALF:HALF], look_up(store[1], slot_sb, V1, S), COPY)
         nc.vector.tensor_tensor(new0_lo[:], acc0[0][:], old0[0][:], MAX)
-        nc.scalar.activation(by_slot(0, 0, HALF), new0_lo[:], COPY)
-        nc.vector.tensor_copy(old1_v[:], by_slot(1, 0, V1))
-        nc.vector.tensor_tensor(new1[:, V1:S], acc1[:, V1:S], old1_s[:], MAX)
-        nc.vector.tensor_tensor(new1[:, 0:V1], acc1[:, 0:V1], old1_v[:], MAX)
+        nc.scalar.activation(look_up(store[0], slot_sb, 0, HALF), new0_lo[:], COPY)
+        nc.vector.tensor_copy(old1_hi[:, 0:V1 - HALF], look_up(store[1], slot_sb, HALF, V1))
+        nc.vector.tensor_copy(old1_lo[:], look_up(store[1], slot_sb, 0, HALF))
+        nc.vector.tensor_tensor(new1[:, HALF:S], acc1[1][:], old1_hi[:], MAX)
+        nc.vector.tensor_tensor(new1[:, 0:HALF], acc1[0][:], old1_lo[:], MAX)
         new0_hi = keep.tile([P, HALF], F32, name="new0_hi", tag="turn")
         nc.vector.tensor_tensor(new0_hi[:], acc0[1][:], old0[1][:], MAX)
-        nc.scalar.activation(by_slot(0, HALF, S), new0_hi[:], COPY)
+        nc.scalar.activation(look_up(store[0], slot_sb, HALF, S), new0_hi[:], COPY)
         nc.sync.dma_start(out[0:P, :], store[0][:])
-        nc.vector.tensor_copy(by_slot(1, 0, S), new1[:])
+        nc.vector.tensor_copy(look_up(store[1], slot_sb, 0, S), new1[:])
         nc.scalar.dma_start(out[P:2 * P, :], store[1][:])

@@ -20,7 +20,7 @@ MAX = mybir.AluOpType.max
 def tile_picked_idxput_max_e_kernel(tc, xT, mem, w1_words, w1_scales, offs, slot, out):
     nc = tc.nc
     HALF = S // 2
-    EDGE = S // 4
+    LOW, HIGH = 192, 384
     COPIED = 896
     V1 = 352
     with ExitStack() as ctx:
@@ -64,17 +64,19 @@ def tile_picked_idxput_max_e_kernel(tc, xT, mem, w1_words, w1_scales, offs, slot
         load_words(1)
         nc.sync.dma_start(store[0][:, COPIED:U], mem[0:P, COPIED:U])
 
-        edges = ((0, EDGE), (S - EDGE, S))
         halves = ((0, HALF), (HALF, S))
-        flat = [[keep.tile([P, 2, EDGE], BF16, name=f"flat{u}_{e}") for e in range(2)] for u in range(2)]
+        own = ((0, LOW), (HIGH, S))
+        rest = ((LOW, HALF), (HALF, HIGH))
         for u in range(2):
+            flat = [keep.tile([P, 2, hi - lo], BF16, name=f"flat{u}_{e}") for e, (lo, hi) in enumerate(rest)]
             for i in range(2):
                 j = 2 * u + i
-                nc.vector.tensor_copy(picked[:, EDGE:S - EDGE, j], look_up(row[j], offs_sb, EDGE, S - EDGE))
-                for e, (lo, hi) in enumerate(edges):
-                    nc.scalar.activation(flat[u][e][:, i, :], look_up(row[j], offs_sb, lo, hi), COPY)
-            for e, (lo, hi) in enumerate(edges):
-                nc.vector.tensor_copy(picked[:, lo:hi, 2 * u:2 * u + 2], flat[u][e][:].rearrange("p j s -> p s j"))
+                for lo, hi in own:
+                    nc.vector.tensor_copy(picked[:, lo:hi, j], look_up(row[j], offs_sb, lo, hi))
+                for e, (lo, hi) in enumerate(rest):
+                    nc.scalar.activation(flat[e][:, i, :], look_up(row[j], offs_sb, lo, hi), COPY)
+            for e, (lo, hi) in enumerate(rest):
+                nc.scalar.activation(picked[:, lo:hi, 2 * u:2 * u + 2], flat[e][:].rearrange("p j s -> p s j"), COPY)
 
         x_codes = [keep.tile([P, HALF], U32, name=f"x_codes{h}", align_bytes=64) for h in range(2)]
         for h, (lo, hi) in enumerate(halves):

@@ -22,7 +22,7 @@ def tile_picked_idxput_max_e_kernel(tc, xT, mem, w1_words, w1_scales, offs, slot
     HALF = S // 2
     LOW, HIGH = 192, 384
     COPIED = 896
-    V1 = 352
+    V1 = 416
     with ExitStack() as ctx:
         keep = ctx.enter_context(tc.tile_pool(name="keep", bufs=1))
         psum = ctx.enter_context(tc.psum_pool(name="psum", bufs=1))

@@ -22,7 +22,7 @@ def tile_picked_idxput_max_e_kernel(tc, xT, mem, w1_words, w1_scales, offs, slot
     HALF = S // 2
     LOW, HIGH = 192, 384
     COPIED = 896
-    V1 = 416
+    V1 = 384
     with ExitStack() as ctx:
         keep = ctx.enter_context(tc.tile_pool(name="keep", bufs=1))
         psum = ctx.enter_context(tc.psum_pool(name="psum", bufs=1))
@@ -58,8 +58,8 @@ def tile_picked_idxput_max_e_kernel(tc, xT, mem, w1_words, w1_scales, offs, slot
         for j in range(1, 4):
             nc.sync.dma_start(row[j][:], xv[:, j, :])
         nc.sync.dma_start(slot_sb[:], slot)
-        load_words(0)
         nc.sync.dma_start(table0[:], mem[0:P, :])
+        load_words(0)
         nc.sync.dma_start(store[1][:], mem[P:2 * P, :])
         load_words(1)
         nc.sync.dma_start(store[0][:, COPIED:U], mem[0:P, COPIED:U])

@@ -37,28 +37,32 @@ def tile_picked_idxput_max_e_kernel(tc, xT, mem, w1_words, w1_scales, offs, slot
         picked = keep.tile([P, S, 4], BF16, name="picked", align_bytes=64)
         x_scale = keep.tile([P, S], U8, name="x_scale", align_bytes=64)
 
+        xv = xT.rearrange("(p j) t -> p j t", j=4)
+        nc.sync.dma_start(offs_sb[:], offs)
+        nc.sync.dma_start(slot_sb[:], slot)
+        nc.scalar.dma_start(row[0][:], xv[:, 0, :])
+
         warm = keep.tile([P, 2], F32, name="warm")
         nc.vector.memset(warm[:, 0:1], 0.0)
         nc.scalar.activation(warm[:, 1:2], warm[:, 0:1], COPY)
 
-        for q in range(4):
-            nc.scalar.dma_start(w_scale[32 * q:32 * q + 4, :].bitcast(I32), w1_scales[0, 4 * q:4 * q + 4, :].bitcast(I32))
-
-        xv = xT.rearrange("(p j) t -> p j t", j=4)
         w_words = w1_words[0].rearrange("p n t -> p (n t)").bitcast(I32)
 
         def look_up(window, offsets, lo, hi):
             return window[:].indirect(offsets[:, lo // 16:hi // 16])
 
+        def load_scales(q):
+            nc.sync.dma_start(w_scale[32 * q:32 * q + 4, :].bitcast(I32), w1_scales[0, 4 * q:4 * q + 4, :].bitcast(I32))
+
         def load_words(b):
             nc.sync.dma_start(w_codes[b][:].bitcast(I32), w_words[:, b * P:(b + 1) * P])
 
-        nc.sync.dma_start(row[0][:], xv[:, 0, :])
-        nc.sync.dma_start(offs_sb[:], offs)
+        for q in range(3):
+            load_scales(q)
         for j in range(1, 4):
             nc.sync.dma_start(row[j][:], xv[:, j, :])
-        nc.sync.dma_start(slot_sb[:], slot)
         nc.sync.dma_start(table0[:], mem[0:P, :])
+        load_scales(3)
         load_words(0)
         nc.sync.dma_start(store[1][:], mem[P:2 * P, :])
         load_words(1)

@@ -22,7 +22,7 @@ def tile_picked_idxput_max_e_kernel(tc, xT, mem, w1_words, w1_scales, offs, slot
     HALF = S // 2
     LOW, HIGH = 192, 384
     COPIED = 896
-    V1 = 384
+    V1 = 352
     with ExitStack() as ctx:
         keep = ctx.enter_context(tc.tile_pool(name="keep", bufs=1))
         psum = ctx.enter_context(tc.psum_pool(name="psum", bufs=1))

@@ -80,7 +80,7 @@ def tile_picked_idxput_max_e_kernel(tc, xT, mem, w1_words, w1_scales, offs, slot
                 for e, (lo, hi) in enumerate(rest):
                     nc.scalar.activation(flat[e][:, i, :], look_up(row[j], offs_sb, lo, hi), COPY)
             for e, (lo, hi) in enumerate(rest):
-                nc.scalar.activation(picked[:, lo:hi, 2 * u:2 * u + 2], flat[e][:].rearrange("p j s -> p s j"), COPY)
+                nc.scalar.copy(picked[:, lo:hi, 2 * u:2 * u + 2], flat[e][:].rearrange("p j s -> p s j"))
 
         x_codes = [keep.tile([P, HALF], U32, name=f"x_codes{h}", align_bytes=64) for h in range(2)]
         for h, (lo, hi) in enumerate(halves):

@@ -29,7 +29,7 @@ def tile_picked_idxput_max_e_kernel(tc, xT, mem, w1_words, w1_scales, offs, slot
 
         offs_sb = keep.tile([P, S // 16], U16, name="offs_sb")
         slot_sb = keep.tile([P, S // 16], U16, name="slot_sb")
-        w_codes = [keep.tile([P, P], U32, name=f"w_codes{b}", align_bytes=64) for b in range(2)]
+        w_codes = keep.tile([P, N], U32, name="w_codes", align_bytes=64)
         w_scale = keep.tile([P, N], U8, name="w_scale", align_bytes=64)
         row = [keep.tile([P, T], F32, name=f"row{j}") for j in range(4)]
         table0 = keep.tile([P, U], F32, name="table0")
@@ -54,18 +54,14 @@ def tile_picked_idxput_max_e_kernel(tc, xT, mem, w1_words, w1_scales, offs, slot
         def load_scales(q):
             nc.sync.dma_start(w_scale[32 * q:32 * q + 4, :].bitcast(I32), w1_scales[0, 4 * q:4 * q + 4, :].bitcast(I32))
 
-        def load_words(b):
-            nc.sync.dma_start(w_codes[b][:].bitcast(I32), w_words[:, b * P:(b + 1) * P])
-
         for q in range(3):
             load_scales(q)
         for j in range(1, 4):
             nc.sync.dma_start(row[j][:], xv[:, j, :])
         nc.sync.dma_start(table0[:], mem[0:P, :])
         load_scales(3)
-        load_words(0)
+        nc.sync.dma_start(w_codes[:].bitcast(I32), w_words)
         nc.sync.dma_start(store[1][:], mem[P:2 * P, :])
-        load_words(1)
         nc.sync.dma_start(store[0][:, COPIED:U], mem[0:P, COPIED:U])
 
         halves = ((0, HALF), (HALF, S))
@@ -89,7 +85,7 @@ def tile_picked_idxput_max_e_kernel(tc, xT, mem, w1_words, w1_scales, offs, slot
 
         def product(dst, b, h):
             lo, hi = halves[h]
-            nc.tensor.matmul_mx(out=dst, lhsT=w_codes[b][:].bitcast(FP8X4),
+            nc.tensor.matmul_mx(out=dst, lhsT=w_codes[:, b * P:(b + 1) * P].bitcast(FP8X4),
                                 lhsT_scale=w_scale[:, b * P:(b + 1) * P],
                                 rhs=x_codes[h][:].bitcast(FP8X4), rhs_scale=x_scale[:, lo:hi],
                                 start=True, stop=True)

from contextlib import ExitStack

import concourse.mybir as mybir

K, T, S, N, U = 512, 1024, 512, 256, 1024
P = 128
FLOPS = 2 * K * S * N

F32 = mybir.dt.float32
BF16 = mybir.dt.bfloat16
I32 = mybir.dt.int32
U32 = mybir.dt.uint32
U16 = mybir.dt.uint16
U8 = mybir.dt.uint8
FP8X4 = mybir.dt.float8_e4m3fn_x4
COPY = mybir.ActivationFunctionType.Copy
MAX = mybir.AluOpType.max


def tile_picked_idxput_max_e_kernel(tc, xT, mem, w1_words, w1_scales, offs, slot, out):
    nc = tc.nc
    HALF = S // 2
    LOW, HIGH = 192, 384
    COPIED = 896
    V1 = 352
    with ExitStack() as ctx:
        keep = ctx.enter_context(tc.tile_pool(name="keep", bufs=1))
        psum = ctx.enter_context(tc.psum_pool(name="psum", bufs=1))

        offs_sb = keep.tile([P, S // 16], U16, name="offs_sb")
        slot_sb = keep.tile([P, S // 16], U16, name="slot_sb")
        w_codes = keep.tile([P, N], U32, name="w_codes", align_bytes=64)
        w_scale = keep.tile([P, N], U8, name="w_scale", align_bytes=64)
        row = [keep.tile([P, T], F32, name=f"row{j}") for j in range(4)]
        table0 = keep.tile([P, U], F32, name="table0")
        store = [keep.tile([P, U], F32, name=f"store{b}") for b in range(2)]
        picked = keep.tile([P, S, 4], BF16, name="picked", align_bytes=64)
        x_scale = keep.tile([P, S], U8, name="x_scale", align_bytes=64)

        xv = xT.rearrange("(p j) t -> p j t", j=4)
        nc.sync.dma_start(offs_sb[:], offs)
        nc.sync.dma_start(slot_sb[:], slot)
        nc.scalar.dma_start(row[0][:], xv[:, 0, :])

        warm = keep.tile([P, 2], F32, name="warm")
        nc.vector.memset(warm[:, 0:1], 0.0)
        nc.scalar.activation(warm[:, 1:2], warm[:, 0:1], COPY)

        w_words = w1_words[0].rearrange("p n t -> p (n t)").bitcast(I32)

        def look_up(window, offsets, lo, hi):
            return window[:].indirect(offsets[:, lo // 16:hi // 16])

        def load_scales(q):
            nc.sync.dma_start(w_scale[32 * q:32 * q + 4, :].bitcast(I32), w1_scales[0, 4 * q:4 * q + 4, :].bitcast(I32))

        for q in range(3):
            load_scales(q)
        for j in range(1, 4):
            nc.sync.dma_start(row[j][:], xv[:, j, :])
        nc.sync.dma_start(table0[:], mem[0:P, :])
        load_scales(3)
        nc.sync.dma_start(w_codes[:].bitcast(I32), w_words)
        nc.sync.dma_start(store[1][:], mem[P:2 * P, :])
        nc.sync.dma_start(store[0][:, COPIED:U], mem[0:P, COPIED:U])

        halves = ((0, HALF), (HALF, S))
        own = ((0, LOW), (HIGH, S))
        rest = ((LOW, HALF), (HALF, HIGH))
        for u in range(2):
            flat = [keep.tile([P, 2, hi - lo], BF16, name=f"flat{u}_{e}") for e, (lo, hi) in enumerate(rest)]
            for i in range(2):
                j = 2 * u + i
                for lo, hi in own:
                    nc.vector.tensor_copy(picked[:, lo:hi, j], look_up(row[j], offs_sb, lo, hi))
                for e, (lo, hi) in enumerate(rest):
                    nc.scalar.activation(flat[e][:, i, :], look_up(row[j], offs_sb, lo, hi), COPY)
            for e, (lo, hi) in enumerate(rest):
                nc.scalar.copy(picked[:, lo:hi, 2 * u:2 * u + 2], flat[e][:].rearrange("p j s -> p s j"))

        x_codes = [keep.tile([P, HALF], U32, name=f"x_codes{h}", align_bytes=64) for h in range(2)]
        for h, (lo, hi) in enumerate(halves):
            nc.vector.quantize_mx(out=x_codes[h][:].bitcast(FP8X4), scales=x_scale[:, lo:hi],
                                  in_=picked[:, lo:hi, :].rearrange("p s j -> p (s j)"))

        def product(dst, b, h):
            lo, hi = halves[h]
            nc.tensor.matmul_mx(out=dst, lhsT=w_codes[:, b * P:(b + 1) * P].bitcast(FP8X4),
                                lhsT_scale=w_scale[:, b * P:(b + 1) * P],
                                rhs=x_codes[h][:].bitcast(FP8X4), rhs_scale=x_scale[:, lo:hi],
                                start=True, stop=True)

        acc0 = [psum.tile([P, HALF], F32, name=f"acc0_{h}") for h in range(2)]
        acc1 = [psum.tile([P, HALF], F32, name=f"acc1_{h}") for h in range(2)]
        for h in range(2):
            product(acc0[h][:], 0, h)
        for h in (1, 0):
            product(acc1[h][:], 1, h)

        old0 = [keep.tile([P, HALF], F32, name=f"old0_{h}") for h in range(2)]
        old1_hi = keep.tile([P, HALF], F32, name="old1_hi", tag="turn")
        old1_lo = keep.tile([P, HALF], F32, name="old1_lo")
        new1 = keep.tile([P, S], F32, name="new1")
        new0_lo = keep.tile([P, HALF], F32, name="new0_lo")
        nc.vector.tensor_copy(store[0][:, 0:COPIED], table0[:, 0:COPIED])
        for h, (lo, hi) in enumerate(halves):
            nc.scalar.activation(old0[h][:], look_up(table0, slot_sb, lo, hi), COPY)
        nc.scalar.activation(old1_hi[:, V1 - HALF:HALF], look_up(store[1], slot_sb, V1, S), COPY)
        nc.vector.tensor_tensor(new0_lo[:], acc0[0][:], old0[0][:], MAX)
        nc.scalar.activation(look_up(store[0], slot_sb, 0, HALF), new0_lo[:], COPY)
        nc.vector.tensor_copy(old1_hi[:, 0:V1 - HALF], look_up(store[1], slot_sb, HALF, V1))
        nc.vector.tensor_copy(old1_lo[:], look_up(store[1], slot_sb, 0, HALF))
        nc.vector.tensor_tensor(new1[:, HALF:S], acc1[1][:], old1_hi[:], MAX)
        nc.vector.tensor_tensor(new1[:, 0:HALF], acc1[0][:], old1_lo[:], MAX)
        new0_hi = keep.tile([P, HALF], F32, name="new0_hi", tag="turn")
        nc.vector.tensor_tensor(new0_hi[:], acc0[1][:], old0[1][:], MAX)
        nc.scalar.activation(look_up(store[0], slot_sb, HALF, S), new0_hi[:], COPY)
        nc.sync.dma_start(out[0:P, :], store[0][:])
        nc.vector.tensor_copy(look_up(store[1], slot_sb, 0, S), new1[:])
        nc.scalar.dma_start(out[P:2 * P, :], store[1][:])
